import numpy as np, ml_dtypes
CORES = [23,119,17,113]
N = 4
BF = ml_dtypes.bfloat16
V, M, C, B, VIS, H, ST = 4096, 256, 2048, 16, 6, 9, 1
def pack(v, words, rel, om, th):
    return {"x": np.ascontiguousarray(v.reshape(N, 128, V)).astype(np.float32).astype(BF), "wd": np.ascontiguousarray(words.reshape(N, 128, M)).astype(np.int32),
            "rt": np.ascontiguousarray(rel.reshape(N, 128, C)).astype(np.int32), "wt": np.ascontiguousarray(om.reshape(N, 128, 1)).astype(np.int32), "th": np.ascontiguousarray(th.reshape(N, 128, 1)).astype(np.int32)}
def setup_inputs(rng):
    return pack(rng.integers(0, 256, (N, 8, 16, V)), rng.integers(0, V, (N, 8, 16, M)), rng.integers(0, V, (N, 8, 16, C)), rng.integers(0, 4096, (N, 8, 16)), rng.integers(1500, 1751, (N, 8, 16)))
def setup_inputs_spread(rng):
    v = np.floor(256 * rng.random((N, 8, 16, V)) * np.exp2(-8 * rng.random((N, 8, 1, V)))).astype(np.int64)
    om = np.floor(4096 * np.exp2(-12.5 * rng.random((N, 8, 16)))).astype(np.int64)
    lev = rng.choice(np.array([300, 700, 1200, 2500, 4080]), (N, 8, 1)); th = np.floor(lev * (0.6 + 0.4 * rng.random((N, 8, 16)))).astype(np.int64)
    pw = rng.choice(np.array([1.0, 1.5, 2.0, 3.0]), (N, 8, 1, 1))
    words = np.floor(V * rng.random((N, 8, 16, M)) ** pw).astype(np.int64); rel = np.floor(V * rng.random((N, 8, 16, C)) ** pw).astype(np.int64)
    return pack(np.minimum(v, 255), np.minimum(words, V - 1), np.minimum(rel, V - 1), np.minimum(om, 4095), np.minimum(th, 4080))
def setup_inputs_ends(rng):
    v = 255 * rng.integers(0, 2, (N, 8, 16, V)); full = rng.random((N, 8)) < 0.5; full[:, 6:] = True
    v[full, :, V - 16:] = 255; v[full, :, 0] = 0
    om = 4095 * rng.integers(0, 2, (N, 8, 16))
    for q in range(N):
        a = 7 - (N - 1 - q) % 2; om[q, 6:] = 4095; om[q, 13 - a, 15] = 272
    hit = [((u * u >> 5) + 37 * u) & (C - 1) for u in (0, 16, 4095)]
    words = (V - 1) * rng.integers(0, 2, (N, 8, 16, M)); mix = rng.random((N, 8, 1, M)) < 0.2; mix[..., 0] = False; mix[..., M - 1] = False
    words = np.where(mix, rng.integers(0, V, (N, 8, 16, M)), words); words[:, :, 0, M - 1] = V - 1; words[:, :, 0, 0] = 0
    rel = (V - 1) * rng.integers(0, 2, (N, 8, 16, C)); mix = rng.random((N, 8, 1, C)) < 0.2; mix[..., hit] = False
    rel = np.where(mix, rng.integers(0, V, (N, 8, 16, C)), rel)
    rel[:, 6:, :, 0] = V - 16 + np.arange(16)
    for c in hit[1:]:
        rel[:, 6:, :, c] = 0; rel[:, 6:, 6, c] = V - 1; rel[:, 6:, 15, c] = V - 1
    pre = rng.choice(np.array([0, 4, H - 1, H, 12, 16]), (N, 8)); pre[:, 0] = 0; pre[:, 6] = 12; pre[:, 7] = 16
    th = 4080 * (np.arange(16) < pre[:, :, None]).astype(np.int64)
    for q in range(N):
        if (N - 1 - q) % 2 == 1:
            th[q, 7, 15] = 4079; th[q, 6, H - 1] = 4079
        else:
            th[q, 6, 11] = 4079
    return pack(v, words, rel, om, th)
def setup_inputs_corners(rng):
    val = np.array([0, 8, 9, 247, 248, 249]); cls = rng.choice(6, (N, 8, V), p=[0.4, 0.1, 0.1, 0.1, 0.2, 0.1])
    cls[:, ::2, 0] = 0; cls[:, 1::2, 0] = 4; cls[:, ::2, V - 1] = 4; cls[:, 1::2, V - 1] = 0
    ft = rng.integers(0, 16, (N, 8, 1, V)); v = rng.integers(0, 7, (N, 8, 16, 1)) + np.where(np.arange(16).reshape(16, 1) == ft, val[cls][:, :, None, :], 0)
    cnt = np.array([31, 8 * M, 33, 0, 63, 32, 1, 64]); order = rng.permutation(N); kk = np.arange(16).reshape(16, 1)
    words = np.zeros((N, 8, 16, M), np.int64); rel = np.zeros((N, 8, 16, C), np.int64); om = np.zeros((N, 8, 16), np.int64)
    for q in range(N):
        hit = (rng.permutation(8 * M) < int(cnt[order[q]])).reshape(8, M)
        lw = np.where(hit, rng.choice(np.array([H, 12, 15, 16]), (8, M)), rng.choice(np.array([0, 1, H - 1]), (8, M)))
        for g in range(8):
            z = np.flatnonzero(cls[q, g] == 0); b = np.flatnonzero(cls[q, g] != 0)
            za = z[rng.integers(0, len(z), (16, M))]; bb = b[rng.integers(0, len(b), (16, M))]
            words[q, g] = np.where(kk < lw[g], za, np.where(kk == lw[g], bb, rng.integers(0, V, (16, M))))
            rel[q, g] = z[rng.integers(0, len(z), (16, C))]
            m = (q + g) % 4
            if m == 1: om[q, g, int(rng.integers(0, 16))] = 4095
            if m == 2: om[q, g] = 4095
            if m == 3: om[q, g] = rng.integers(0, 4096, 16)
    return pack(v, words, rel, om, rng.choice(np.array([0, 0, 1]), (N, 8, 16)))
def setup_inputs_ties(rng):
    pr = rng.integers(0, 256, (N, 8, 16, 6)); v = np.take_along_axis(pr, rng.integers(0, 6, (N, 8, 1, V)), 3)
    dd = np.sort(np.add.reduce(np.abs(pr[:, :, :, :, None] - pr[:, :, :, None, :]), axis=2).reshape(N, 8, 36), axis=2)
    ix = np.minimum(rng.choice(np.array([20, 28, 33]), (N, 8, 1)) + rng.integers(0, 8, (N, 8, 16)), 35)
    th = np.maximum(np.take_along_axis(dd, ix, 2) - rng.integers(0, 2, (N, 8, 16)), 0)
    words = rng.integers(0, V, (N, 8, 16, M)); words[:, :, :, ::3] = words[:, :, :1, ::3].copy()
    rel = rng.integers(0, V, (N, 8, 16, C)); rel[:, :, :, ::4] = rel[:, :, :1, ::4].copy()
    om = rng.integers(0, 4096, (N, 8, 16))
    for q in range(N):
        for g in range(1, 8, 2):
            b = int(rng.integers(1, V - 2)); a = rng.integers(0, 100, 16)
            v[q, g, :, b] = a; v[q, g, :, b + 1] = a + 150; v[q, g, :, V - 1] = a + 100; v[q, g, :, 0] = a + 100; v[q, g, int(rng.integers(0, 16)), 0] += 1
            u = int(np.add.reduce(om[q, g] * a)) & 4095; c = ((u * u >> 5) + 37 * u) & (C - 1)
            rel[q, g, :, c] = b + 1; rel[q, g, 0, c] = 0; rel[q, g, 15, c] = V - 1
            words[q, g, 0, 1::8] = b; th[q, g, 0] = 1600
    return pack(v, words, rel, om, th)
def setup_inputs_still(rng):
    far = V // 2 + rng.permutation(V // 2)[:V // 4]; zero = rng.permutation(np.setdiff1d(np.arange(V), far))[:V // 4]
    val = rng.choice(np.array([1, 8, 9, 100, 248]), (N, 8, V)); val[..., zero] = 0; val[..., far] = 0
    ft = rng.integers(0, 16, (N, 8, 1, V)); kk = np.arange(16).reshape(16, 1)
    v = rng.integers(0, 7, (N, 8, 16, 1)) + np.where(kk == ft, val[:, :, None, :], 0)
    v[:, :, 2:5, far] = 255 - rng.integers(0, 7, (N, 8, 3, V // 4))
    words = np.where((kk + rng.integers(0, 4, (N, 8, 1, M))) % 4 == 0, far[rng.integers(0, V // 4, (N, 8, 16, M))], rng.integers(0, V, (N, 8, 16, M)))
    rel = zero[rng.integers(0, V // 4, (N, 8, 16, C))]
    cnt = rng.permutation(np.array([1, 31, 33, 63])); par = int(rng.integers(0, 2))
    for q in range(par, N, 2):
        hit = np.zeros((8, M), bool); hit[:, :M // 2] = (rng.permutation(8 * (M // 2)) < int(cnt[q // 2])).reshape(8, M // 2)
        lw = rng.choice(np.array([H, 12, 16]), (8, 1, M))
        w = np.where(kk < lw, zero[rng.integers(0, V // 4, (8, 16, M))], far[rng.integers(0, V // 4, (8, 16, M))])
        words[q] = np.where(hit[:, None, :], w, words[q])
    return pack(v, words, rel, rng.integers(0, 4096, (N, 8, 16)), rng.choice(np.array([0, 0, 1]), (N, 8, 16)))
def check_inputs(d):
    bad = []
    for k, hi in (("x", 255), ("wd", V - 1), ("rt", V - 1), ("wt", 4095), ("th", 4080)):
        v = np.asarray(d[k]).astype(np.float64)
        if not (np.min(v) >= 0 and np.max(v) <= hi): bad.append("range of " + k)
        elif np.any(v != np.floor(v)): bad.append("whole numbers of " + k)
    return bad
def reference(x, wd, rt, wt, th):
    X = x.astype(np.float32).astype(np.int32).reshape(N, 8, 16, V)
    W = wd.astype(np.int64).reshape(N, 8, 16, M); RT = rt.astype(np.int64).reshape(N, 8, 16, C)
    om = wt.astype(np.int64).reshape(N, 8, 16, 1); lim = th.astype(np.int64).reshape(N, 8, 16, 1)
    A = np.zeros(N, np.int64); k = np.arange(16).reshape(1, 1, 16, 1); i = np.arange(M).reshape(1, 1, M)
    def pick(c):
        return np.take_along_axis(X, c.reshape(N, 8, 1, 16 * M), 3).reshape(N, 8, 16, 16, M)
    for t in range(VIS):
        if t > 0:
            W = np.roll(np.roll(W, ST, axis=0), (t + t // N) - (t - 1 + (t - 1) // N), axis=1)
        xw = pick(W); x0 = xw[:, :, :, 0]
        u = np.add.reduce(om * x0, axis=2) & 4095
        c = ((u * u >> 5) + 37 * u) & (C - 1)
        R = np.take_along_axis(RT, c[:, :, None, :], 3)
        s = np.argmin(np.add.reduce(np.abs(pick(R) - x0[:, :, :, None, :]), axis=2), axis=2)
        Q = np.take_along_axis(R, (s[:, :, None, :] + k) & 15, 2)
        xq = pick(Q); gap = np.add.reduce(np.abs(xw - xq), axis=2)
        ok = (gap <= lim + 8 * (A & 31).reshape(N, 1, 1, 1)).astype(np.int64)
        l = np.add.reduce(np.minimum.accumulate(ok, axis=2), axis=2)[:, :, None, :]
        rep = l >= H; uu = u[:, :, None, :]
        new = np.where(k < 16 - l, Q[:, :, ::-1] ^ 1, np.where(k < 32 - 2 * l, np.take_along_axis(W, (k + 2 * l - 16) & 15, 2), ((Q * uu >> 5) + Q) & (V - 1)))
        W = np.where(rep, new, np.take_along_axis(W, (k + l + 1) & 15, 2))
        at = (B * i + (u & (B - 1)))[:, :, None, :]
        np.put_along_axis(X, at, np.where(rep, (x0 + xq[:, :, :, 15]) >> 1, np.take_along_axis(X, at, 3)), 3)
        A = np.add.reduce(rep.reshape(N, 8 * M).astype(np.int64), axis=1)
    return {"yx": X.reshape(N, 128, V).astype(np.float32).astype(BF), "yw": W.reshape(N, 128, M).astype(np.float32)}

@@ -1,0 +1,567 @@
+from concourse.mybir import dt, AluOpType as OP, AxisListType, ActivationFunctionType as AF
+
+VIS = 6
+NC = 2
+CW = 128
+TURNS = (1, 2, 3, 4, 5, 6, 7, 8, 9, 10, 12, 14, 16)
+
+ORDER = """
+a.wcopy a.gather_w:1v a.gather_w:0s a.weigh a.relator b.gather_w:1s a.spread b.gather_w:0v a.gather_r:0 b.wcopy a.letters a.gather_r:1
+b.weigh a.spin:2 a.tail a.biggest:0 b.spin:0 a.keys_r b.relator a.biggest:1 a.keys_m b.gather_r:0 b.spin:2 b.letters b.gather_r:1
+a.least a.spin:1 a.pwin a.gather_q:1 b.spread a.gather_q:0 allow b.tail b.biggest:9 a.turn_list b.keys_r a.sizes:0 b.keys_m a.sizes:1
+b.least b.spin:3 a.spin:3 a.match a.spin:0 b.gather_q:0 a.moves a.turned b.gather_q:1 a.halves b.pwin a.unpack b.turn_list b.sizes:0
+a.renew b.sizes:1 b.spin:1 b.match b.moves a.write_x a.tally b.unpack b.turned b.renew b.halves b.tally b.write_x
+"""
+FIRST = """
+constants_1 constants_3 a.gather_w:0v a.gather_w:1s b.gather_w:1s a.weigh a.relator b.gather_w:0s a.wcopy a.gather_r:0 tables b.weigh
+a.biggest:0 a.gather_r:1 b.relator rows a.biggest:1 a.keys_r a.keys_m a.least b.gather_r:1 turns b.spread b.wcopy a.spread b.gather_r:0
+b.spin:2 constants_2 a.gather_q:0 a.spin:0 a.letters a.tail b.letters b.keys_r a.turn_list b.biggest:9 a.spin:1 a.gather_q:1 b.spin:0
+a.pwin b.keys_m a.spin:2 b.least a.halves a.sizes:1 a.sizes:0 b.spin:3 b.tail a.match a.spin:3 a.moves b.pwin b.gather_q:0 b.turn_list
+b.sizes:0 b.gather_q:1 a.tally a.turned b.halves a.unpack a.renew b.sizes:1 b.match b.spin:1 b.moves a.write_x b.unpack b.turned b.tally
+b.renew b.write_x
+"""
+
+SCRATCH = {
+    "xs": ("sbuf", [128, 4352], "bfloat16"),
+    "rts": ("sbuf", [128, 2048], "int32"),
+    "wdi": ("sbuf", [128, 256], "int32"),
+    "wti": ("sbuf", [128, 2], "int32"),
+    "thi": ("sbuf", [128, 2], "int32"),
+    "wl": ("sbuf", [128, 256 * VIS], "uint16"),
+    "wo": ("sbuf", [128, 256 * VIS], "uint16"),
+    "ywf": ("sbuf", [128, 256], "float32"),
+    "nvi": ("sbuf", [128, 256], "int32"),
+    "ones": ("sbuf", [128, 256], "bfloat16"),
+    "zerf": ("sbuf", [128, 128], "float32"),
+    "blk": ("sbuf", [128, 128], "bfloat16"),
+    "blk0": ("sbuf", [128, 128], "bfloat16"),
+    "i2": ("sbuf", [128, 256], "bfloat16"),
+    "an2": ("sbuf", [128, 256], "bfloat16"),
+    "i2h": ("sbuf", [128, 256], "float16"),
+    "an2h": ("sbuf", [128, 256], "float16"),
+    "hid": ("sbuf", [128, 128], "bfloat16"),
+    "tri": ("sbuf", [128, 128], "bfloat16"),
+    "m3": ("sbuf", [128, 128], "bfloat16"),
+    "e8": ("sbuf", [128, 128], "bfloat16"),
+    "m1a": ("sbuf", [128, 128], "bfloat16"),
+    "m1": ("sbuf", [128, 128], "bfloat16"),
+    "m2a": ("sbuf", [128, 128], "bfloat16"),
+    "m2b": ("sbuf", [128, 128], "bfloat16"),
+    "m2": ("sbuf", [128, 128], "bfloat16"),
+    "g8": ("sbuf", [128, 128], "float32"),
+    "b0": ("sbuf", [128, 144], "bfloat16"),
+    "c0": ("sbuf", [128, 144], "bfloat16"),
+    "rot": ("sbuf", [128, 1664], "float16"),
+    "mdd": ("sbuf", [128, 160], "bfloat16"),
+    "kt2": ("sbuf", [128, 160], "bfloat16"),
+    "m1b": ("sbuf", [128, 128], "bfloat16"),
+    "tabr": ("sbuf", [128, 2048], "float32"),
+    "tabc": ("sbuf", [128, 2048], "float32"),
+    "tabi": ("sbuf", [128, 2048], "int32"),
+    "rota": ("sbuf", [128, 1664], "bfloat16"),
+    "rotb": ("sbuf", [128, 1664], "bfloat16"),
+    "bm": ("sbuf", [128, 2048], "bfloat16"),
+    "bmh": ("sbuf", [128, 2048], "float16"),
+    "k2h": ("sbuf", [128, 128], "float16"),
+    "oneh": ("sbuf", [128, 128], "float16"),
+    "y0": ("sbuf", [128, 8], "float16"),
+    "y1": ("sbuf", [128, 8], "float16"),
+    "wt0": ("sbuf", [128, 144], "float16"),
+    "wb": ("sbuf", [128, 128], "float16"),
+    "s32": ("sbuf", [128, 8], "bfloat16"),
+    "s16": ("sbuf", [128, 8], "bfloat16"),
+    "s128": ("sbuf", [128, 8], "bfloat16"),
+    "kt": ("sbuf", [128, 128], "bfloat16"),
+    "row16": ("sbuf", [128, 128], "bfloat16"),
+    "md": ("sbuf", [128, 128], "bfloat16"),
+    "rs": ("sbuf", [128, 128], "float32"),
+    "keep": ("sbuf", [128, 128], "bfloat16"),
+    "pi": ("sbuf", [128, 2], "int32"),
+    "pj": ("sbuf", [128, 2], "int32"),
+    "cols": ("sbuf", [128, 64], "float32"),
+    "ihi": ("sbuf", [128, 8], "float32"),
+    "it": ("sbuf", [128, 8], "bfloat16"),
+    "m128": ("sbuf", [128, 8], "bfloat16"),
+    "itg": ("sbuf", [128, 16], "float32"),
+    "itf": ("sbuf", [128, 16], "float32"),
+    "ite": ("sbuf", [128, 16], "float32"),
+    "itd": ("sbuf", [128, 16], "float32"),
+    "cnt": ("sbuf", [128, 2], "float32"),
+    "ai": ("sbuf", [128, 2], "int32"),
+    "aj": ("sbuf", [128, 2], "int32"),
+}
+for _c in range(NC):
+    SCRATCH.update({
+        "xw%d" % _c: ("sbuf", [128, 2048], "bfloat16"),
+        "xr%d" % _c: ("sbuf", [128, 2048], "bfloat16"),
+        "mx%d" % _c: ("sbuf", [128, 2048], "bfloat16"),
+        "df%d" % _c: ("sbuf", [128, 2048], "bfloat16"),
+        "ww%d" % _c: ("sbuf", [128, 1664], "float32"),
+        "pw%d" % _c: ("sbuf", [128, 2048], "float32"),
+        "wf%d" % _c: ("sbuf", [128, 128], "float16"),
+        "pk%d" % _c: ("sbuf", [128, 128], "float32"),
+        "dp%d" % _c: ("dram", [8, 32, 128], "float32"),
+        "x0%d" % _c: ("sbuf", [128, 128], "float16"),
+        "ti%d" % _c: ("sbuf", [128, 1024], "int32"),
+        "tf%d" % _c: ("sbuf", [128, 512], "float32"),
+        "ui%d" % _c: ("sbuf", [128, 64], "int32"),
+        "uf%d" % _c: ("sbuf", [128, 64], "float32"),
+        "ls%d" % _c: ("sbuf", [128, 64], "uint16"),
+        "r16%d" % _c: ("sbuf", [128, 128], "uint16"),
+        "l2%d" % _c: ("sbuf", [128, 128], "uint16"),
+        "sc%d" % _c: ("sbuf", [128, 128], "float32"),
+        "zs%d" % _c: ("sbuf", [128, 128], "bfloat16"),
+        "sb%d" % _c: ("sbuf", [128, 384], "bfloat16"),
+        "pp%d" % _c: ("sbuf", [128, 384], "bfloat16"),
+        "tl%d" % _c: ("sbuf", [128, 128], "int32"),
+        "ff%d" % _c: ("sbuf", [128, 384], "float32"),
+        "ph%d" % _c: ("sbuf", [128, 384], "float16"),
+    })
+for _b in range(8):
+    SCRATCH["ps%d" % _b] = ("psum", [128, 512], "float32")
+
+SEMAPHORES = ["v", "s", "pe", "gp", "sent", "dacc", "ldx", "ldx2", "ldr", "ldw", "ldt", "ldh", "outw", "outx"]
+SEMAPHORES += ["dp%d%d" % (st, c) for st in (1, 2) for c in range(NC)]
+SEMAPHORES += ["ar%d_%d" % (t, c) for t in range(1, VIS) for c in range(NC)]
+
+
+def rank_program(g, core, T, topo):
+    rank = T.rank_of(core)
+    if rank is None:
+        return
+    nrank = len(T.cores)
+    nxt = T.cores[(rank + 1) % nrank]
+    V, S, PE, SY = g.vector, g.scalar, g.tensor, g.sync
+    queue = {"v": V, "s": S, "pe": PE, "gp": g, "sy": SY}
+    total = {}
+    know = {q: {} for q in queue}
+    wrote, seen = {}, {}
+
+    def need(q, tok):
+        if tok is None:
+            return
+        sem, val, clock, _ = tok
+        if know[q].get(sem, 0) < val:
+            queue[q].wait_ge(T.sem[sem], val)
+            for s2, v2 in clock.items():
+                if know[q].get(s2, 0) < v2:
+                    know[q][s2] = v2
+            know[q][sem] = val
+
+    def sync_for(q, reads, writes, banks):
+        toks = []
+        for r in reads:
+            toks.append(wrote[r])
+        for w in writes:
+            if w in wrote and not (q == "pe" and wrote[w][3] == q):
+                toks.append(wrote[w])
+            for tok in seen.get(w, {}).values():
+                if tok[3] != q or q == "sy":
+                    toks.append(tok)
+        for b in banks:
+            for q2, tok in seen.get(b, {}).items():
+                if q2 != q:
+                    toks.append(tok)
+        toks.sort(key=lambda z: -z[1])
+        for tok in toks:
+            need(q, tok)
+
+    def note(q, tok, reads, writes, banks):
+        for w in writes:
+            wrote[w] = tok
+            seen[w] = {}
+        for r in reads:
+            seen.setdefault(r, {})[tok[0]] = tok
+        for b in banks:
+            seen.setdefault(b, {})[q] = tok
+
+    def op(q, call, reads, writes, banks=()):
+        sync_for(q, reads, writes, banks)
+        total[q] = total.get(q, 0) + 1
+        call().then_inc(T.sem[q], 1)
+        note(q, (q, total[q], dict(know[q]), q), reads, writes, banks)
+
+    def dmas(q, calls, sem, reads, writes):
+        sync_for(q, reads, writes, ())
+        for call in calls:
+            total[sem] = total.get(sem, 0) + 16
+            call().then_inc(T.sem[sem], 16)
+        note(q, (sem, total[sem], dict(know[q]), "dma"), reads, writes, ())
+
+    def mm(out, lhsT, rhs, reads, bank, start=True, stop=True, tag=None):
+        op("pe", lambda: PE.matmul(out, lhsT, rhs, start, stop), reads, [tag] if tag else [], [bank])
+
+    def tt(out, a, b, o, reads, writes, banks=()):
+        op("v", lambda: V.tensor_tensor(out, a, b, o), reads, writes, banks)
+
+    def ts(out, a, s1, o1, reads, writes, banks=(), s2=None, o2=None):
+        if o2 is None:
+            op("v", lambda: V.tensor_scalar(out, a, s1, None, o1), reads, writes, banks)
+        else:
+            op("v", lambda: V.tensor_scalar(out, a, s1, s2, o1, o2), reads, writes, banks)
+
+    def cp(out, a, reads, writes, banks=()):
+        op("v", lambda: V.tensor_copy(out, a), reads, writes, banks)
+
+    dmas("sy", [lambda: SY.dma_start(T.wdi[:], T.wd[:])], "ldw", [], ["wdi"])
+    dmas("s", [lambda: S.dma_start(T.xs[:, 0:2048], T.x[:, 0:2048])], "ldx", [], ["x_lo"])
+    dmas("sy", [lambda: SY.dma_start(T.xs[:, 2048:4096], T.x[:, 2048:4096])], "ldx2", [], ["x_hi"])
+    dmas("sy", [lambda: SY.dma_start(T.wti[:, 0:1], T.wt[:])], "ldt", [], ["wti"])
+    dmas("sy", [lambda: SY.dma_start(T.rts[:], T.rt[:])], "ldr", [], ["rts"])
+    dmas("sy", [lambda: SY.dma_start(T.thi[:, 0:1], T.th[:])], "ldh", [], ["thi"])
+
+    def col(n):
+        return T.cols[:, n:n + 1]
+
+    def sel(out, in_, pattern, cmp, fill, base, cm, reads, writes):
+        op("gp", lambda: g.affine_select(out, in_, pattern, cmp, fill, base, cm), reads, writes)
+
+    op("v", lambda: V.memset(T.ones[:], 1.0), [], ["ones"])
+    op("gp", lambda: g.iota(T.pi[:], [[0, 2]], 0, 1), [], ["pi"])
+    sel(T.blk0[:], T.ones[:, 0:128], [[-16, 8], [0, 16]], OP.is_ge, 0.0, 0, 1, ["ones"], ["blk0"])
+    sel(T.blk[:], T.blk0[:], [[16, 8], [0, 16]], OP.is_ge, 0.0, 15, -1, ["blk0"], ["blk"])
+    sel(T.i2[:], T.ones[:], [[0, 2], [-1, 128]], OP.is_equal, 0.0, 0, 1, ["ones"], ["i2"])
+    op("v", lambda: V.memset(T.zerf[:], 0.0), [], ["zerf"])
+    op("v", lambda: V.memset(T.b0[:], 0.0), [], ["b0"])
+    for c in range(NC):
+        op("v", lambda: V.memset(T["zs%d" % c][:], 1.0), [], ["zs%d" % c])
+    ts(T.pj[:], T.pi[:], 15, OP.bitwise_and, ["pi"], ["pj"])
+    cp(col(0), T.pj[:, 0:1], ["pj"], ["k0"])
+    op("gp", lambda: g.iota(T.kt[:], [[0, 8], [1, 16]], 0, 0, allow_small_or_imprecise_dtypes=True), [], ["kt"])
+    sel(T.keep[:], T.ones[:, 0:128], [[0, 8], [1, 16]], OP.not_equal, 0.0, 0, 0, ["ones"], ["keep"])
+    cp(T.b0[:, 15:143:16], T.blk[:, 0:128:16], ["blk"], ["b0"])
+    cp(T.wl[:, 0:256], T.wdi[:], ["wdi"], ["wl0_0", "wl0_1"])
+    cp(col(1), T.wti[:, 0:1], ["wti"], ["w1"])
+    ts(col(2), col(1), 2048.0, OP.is_ge, ["w1"], ["w2"], (), -4096.0, OP.mult)
+    tt(col(3), col(1), col(2), OP.add, ["w1", "w2"], ["w3"])
+    ts(T.wt0[:], T.b0[:], col(3), OP.mult, ["b0", "w3"], ["wt0"])
+    cp(T.i2h[:], T.i2[:], ["i2"], ["i2h"])
+    ts(T.wb[:], T.blk[:], col(3), OP.mult, ["blk", "w3"], ["wb"])
+    ts(T.md[:], T.kt[:], col(0), OP.is_equal, ["kt", "k0"], ["md"])
+    ts(T.k2h[:], T.ones[:, 0:128], 2048.0, OP.mult, ["ones"], ["k2h"])
+    cp(T.oneh[:], T.ones[:, 0:128], ["ones"], ["oneh"])
+
+    def tables():
+        ts(T.tabi[:], T.rts[:], 1, OP.bitwise_and, ["rts"], ["tabi"])
+        ts(T.tabc[:], T.tabi[:], -2.0, OP.mult, ["tabi"], ["tabc"], (), -2047.0, OP.add)
+        cp(T.tabr[:], T.rts[:], ["rts"], ["tabr"])
+        dmas("gp", [lambda: g.dma_start(T.tabc[:], T.tabr[:], accum_op=OP.add)], "dacc", ["tabr", "tabc"], ["tabc"])
+
+    def turns():
+        cp(T.rot[:], T.rotb[:], ["rotb%d" % n for n in range(len(TURNS))], ["rot"])
+
+    def rows():
+        cp(T.bmh[:], T.bm[:], ["bm%d" % n for n in range(8)], ["bmh"])
+
+    def constants_1():
+        sel(T.rs[:], T.zerf[:], [[0, 8], [1, 16]], OP.not_equal, 524288.0, 0, 0, ["zerf"], ["rs"])
+        op("gp", lambda: g.iota(T.row16[:], [[16, 128]], 0, 0, allow_small_or_imprecise_dtypes=True), [], ["row16"])
+        op("gp", lambda: g.iota(T.ihi[:], [[16, 8]], 0, 0, allow_small_or_imprecise_dtypes=True), [], ["ihi"])
+        op("gp", lambda: g.iota(T.itg[:], [[16, 16]], 0, 0, allow_small_or_imprecise_dtypes=True), [], ["itg"])
+        sel(T.tri[:], T.blk[:], [[1, 128]], OP.is_ge, 0.0, 0, -1, ["blk"], ["tri"])
+        sel(T.e8[:], T.ones[:, 0:128], [[-16, 8], [0, 16]], OP.is_equal, 0.0, -8, 1, ["ones"], ["e8"])
+        sel(T.an2[:], T.ones[:], [[0, 2], [-16, 8], [1, 16]], OP.is_equal, 0.0, -15, 1, ["ones"], ["an2"])
+        sel(T.m3[:], T.ones[:, 0:128], [[-16, 8], [1, 8], [0, 2]], OP.is_equal, 0.0, -15, 1, ["ones"], ["m3"])
+        ts(T.s32[:], T.blk[:, 0:128:16], 32.0, OP.mult, ["blk"], ["s32"])
+        ts(T.s16[:], T.blk[:, 0:128:16], -16.0, OP.mult, ["blk"], ["s16"])
+        ts(T.s128[:], T.blk[:, 0:128:16], 128.0, OP.mult, ["blk"], ["s128"])
+        ts(T.m128[:], T.ones[:, 0:8], col(0), OP.mult, ["ones", "k0"], ["m128"], (), -128.0, OP.mult)
+        ts(T.it[:], T.ihi[:], col(0), OP.add, ["ihi", "k0"], ["it"])
+        ts(T.hid[:], T.i2[:, 0:128], 0.5, OP.mult, ["i2"], ["hid"])
+
+    def constants_3():
+        op("gp", lambda: g.iota(T.kt2[:], [[0, 10], [1, 16]], 0, 0, allow_small_or_imprecise_dtypes=True), [], ["kt2"])
+        for n in range(8):
+            sel(T.bm[:, 256 * n:256 * n + 256], T.ones[:], [[-1, 2], [-16, 8], [0, 16]], OP.is_equal, 0.0, -2 * n, 1, ["ones"], ["bm%d" % n])
+        ts(T.mdd[:], T.kt2[:], col(0), OP.is_equal, ["kt2", "k0"], ["mdd"])
+        for n, q in enumerate(TURNS):
+            a = T.rota[:, 128 * n:128 * n + 128]
+            sel(a, T.mdd[:, q:q + 128], [[-16, 8], [0, 16]], OP.is_ge, 0.0, 0, 1, ["mdd"], ["rota%d" % n])
+            sel(T.rotb[:, 128 * n:128 * n + 128], a, [[16, 8], [0, 16]], OP.is_ge, 0.0, 15, -1, ["rota%d" % n], ["rotb%d" % n])
+
+    def constants_2():
+        cp(col(8), T.thi[:, 0:1], ["thi"], ["thf"])
+        ts(col(4), col(0), 1.0, OP.add, ["k0"], ["k1"])
+        ts(T.itf[:], T.itg[:], col(0), OP.add, ["itg", "k0"], ["itf"], (), 4096.0, OP.add)
+        ts(T.itd[:], T.itg[:], col(0), OP.add, ["itg", "k0"], ["itd"], (), 15.0, OP.mult)
+        ts(T.ite[:], T.itd[:], -4096.0, OP.add, ["itd"], ["ite"])
+        ts(col(5), col(0), 8.0, OP.is_equal, ["k0"], ["q8"])
+        ts(col(6), col(0), 9.0, OP.is_ge, ["k0"], ["q9"], (), 1.0, OP.add)
+        ts(col(7), col(5), -8.0, OP.mult, ["q8"], ["q7"])
+        tt(col(11), col(6), col(7), OP.add, ["q9", "q7"], ["qd"])
+        ts(col(12), col(0), 13.0, OP.is_ge, ["k0"], ["q13"])
+        tt(col(9), col(11), col(12), OP.subtract, ["qd", "q13"], ["qc"])
+        ts(T.c0[:], T.b0[:], col(9), OP.mult, ["b0", "qc"], ["c0"], (), 128.0, OP.mult)
+        ts(T.g8[:], T.ones[:, 0:128], col(5), OP.mult, ["ones", "q8"], ["g8"])
+        cp(T.an2h[:], T.an2[:], ["an2"], ["an2h"])
+        tt(T.m1a[:], T.e8[:], T.i2[:, 0:128], OP.subtract, ["e8", "i2"], ["m1a"])
+        tt(T.m2a[:], T.an2[:, 0:128], T.e8[:], OP.subtract, ["an2", "e8"], ["m2a"])
+        sel(T.m1b[:], T.m1a[:], [[0, 8], [1, 16]], OP.is_ge, 0.0, -8, 0, ["m1a"], ["m1b"])
+        ts(T.m1[:], T.m1b[:], 4096.0, OP.mult, ["m1b"], ["m1"])
+        sel(T.m2b[:], T.m2a[:], [[0, 8], [-1, 16]], OP.is_ge, 0.0, 7, 0, ["m2a"], ["m2b"])
+        tt(T.m2[:], T.m2b[:], T.m3[:], OP.subtract, ["m2b", "m3"], ["m2"])
+
+    XR = ["x_lo", "x_hi"]
+
+    def stages(t, c):
+        B = ["ps%d" % (4 * c + b) for b in range(4)]
+        P = [T[b] for b in B]
+        r = lambda name: "%s_%d" % (name, c)
+        xw, xr, mx, df = T["xw%d" % c], T["xr%d" % c], T["mx%d" % c], T["df%d" % c]
+        ti, tf, ui, uf, ls = T["ti%d" % c], T["tf%d" % c], T["ui%d" % c], T["uf%d" % c], T["ls%d" % c]
+        w0 = 256 * t + CW * c
+        wres = "wl%d_%d" % (t, c)
+        TI = lambda n: ti[:, 128 * n:128 * n + 128]
+        TF = lambda n: tf[:, 128 * n:128 * n + 128]
+        UI = lambda n: ui[:, 8 * n:8 * n + 8]
+        UF = lambda n: uf[:, 8 * n:8 * n + 8]
+        LS = lambda n: ls[:, 8 * n:8 * n + 8]
+        last = t == VIS - 1
+
+        def gather_w(h, q):
+            o = xw[:, 1024 * h:1024 * h + 1024]
+            i = T.xs[:, 0:4096].indirect(T.wl[:, w0 + 64 * h:w0 + 64 * h + 64])
+            if q == "s":
+                op("s", lambda: S.activation(o, i, AF.Copy), XR + [wres], [r("xw%d" % h)])
+            else:
+                op("v", lambda: V.tensor_copy(o, i), XR + [wres], [r("xw%d" % h)])
+
+        def wcopy():
+            ts(T["wf%d" % c][:], T.wl[:, w0:w0 + CW], -2048.0, OP.add, [wres], [r("wf")])
+
+        def spin(n):
+            lo, hi = 4 * n, min(4 * n + 4, len(TURNS))
+            for q in range(lo, hi):
+                mm(P[3][:, 128 * (q - lo):128 * (q - lo) + 128], T.rot[:, 128 * q:128 * q + 128], T["wf%d" % c][:],
+                   ["rot", r("wf")], B[3], True, True, r("wsp"))
+            op("s", lambda: S.activation(T["ww%d" % c][:, 128 * lo:128 * hi], P[3][:, 0:128 * (hi - lo)], AF.Copy),
+               [r("wsp")], [r("ww%d" % n)], [B[3]])
+
+        def window(kind, src, win, dram, off):
+            d, w, s = T[dram], T[win], T[src]
+            rs = [r(kind + "f")]
+            dmas("sy", [lambda: SY.dma_start(d[:, 0:16, :], s[:]), lambda: SY.dma_start(d[:, 16:32, :], s[:])],
+                 "d%s1%d" % (kind, c), rs, [r(kind + "d")])
+            dmas("sy", [(lambda k: lambda: SY.dma_start(w[k:128:16, :], d[:, k + off:k + off + 16, :]))(k) for k in range(16)],
+                 "d%s2%d" % (kind, c), [r(kind + "d")], [r(kind + "w")])
+
+        def pwin():
+            window("p", "pk%d" % c, "pw%d" % c, "dp%d" % c, 0)
+
+        def pick(src, srcs, banks, tmp, out):
+            a, b2 = TF(tmp), TF(tmp + 1)
+            tt(a, src, T.md[:], OP.mult, srcs + ["md"], [r("f%d" % tmp)], banks)
+            op("v", lambda: V.tensor_tensor_scan(b2, T.keep[:], a, 0.0, OP.mult, OP.add), ["keep", r("f%d" % tmp)], [r("f%d" % (tmp + 1))])
+            return tf[:, 128 * tmp + 143:128 * tmp + 256:16], r("f%d" % (tmp + 1))
+
+        def weigh():
+            x0 = T["x0%d" % c]
+            cp(x0[:], xw[:, 0:2048:16], [r("xw0"), r("xw1")], [r("x0")])
+            if c == 0:
+                mm(P[1][:, 8:136], T.wb[:], x0[:], ["wb", r("x0")], B[1], True, True, r("ub"))
+            else:
+                for m in range(16):
+                    mm(P[1][:, 0:8], T.wt0[:, 15 - m:143 - m], x0[:, m:128:16], ["wt0", r("x0")], B[1], m == 0, m == 15, r("uw"))
+            mm(P[0][:, 0:128], T.i2h[:, 0:128], x0[:], ["i2h", r("x0")], B[0], True, True, r("x0p"))
+
+        def relator():
+            if c == 0:
+                src, res = pick(P[1][:, 8:136], [r("ub")], [B[1]], 0, None)
+                cp(UI(0), src, [res], [r("u0")])
+            else:
+                cp(UI(0), P[1][:, 0:8], [r("uw")], [r("u0")], [B[1]])
+            ts(UI(1), UI(0), 4095, OP.bitwise_and, [r("u0")], [r("u1")])
+            ts(T["y%d" % c][:], UI(1), -2048.0, OP.add, [r("u1")], [r("y")])
+            ts(UF(1), UI(1), 3232.0, OP.add, [r("u1")], [r("uz")])
+            tt(UI(2), T["y%d" % c][:], UF(1), OP.mult, [r("y"), r("uz")], [r("u2")])
+            ts(UI(3), UI(2), 5, OP.arith_shift_right, [r("u2")], [r("u3")], (), 2047, OP.bitwise_and)
+            cp(LS(0), UI(3), [r("u3")], [r("cl")])
+            cp(T["r16%d" % c][:], T.rts[:].indirect(LS(0)), ["rts", r("cl")], [r("r16")])
+            ts(UI(4), UI(1), 15, OP.bitwise_and, [r("u1")], [r("u4")])
+
+        def spread():
+            y = T["y%d" % c]
+            mm(P[0][:, 384:512], T.k2h[0:1, :], T.oneh[0:1, :], ["k2h", "oneh"], B[0], True, False, r("us"))
+            for m in range(16):
+                mm(P[0][:, 384 + m:512:16], T.bmh[:, 128 * m:128 * m + 128], y[:], ["bmh", r("y")], B[0], False, m == 15, r("us"))
+
+        def letters():
+            op("s", lambda: S.activation(TF(0), T.tabr[:].indirect(LS(0)), AF.Copy), ["tabr", r("cl")], [r("f0")])
+            op("s", lambda: S.activation(TF(1), T.tabc[:].indirect(LS(0)), AF.Copy, scale=1.0 / 4096), ["tabc", r("cl")], [r("f1")])
+
+        def gather_r(h):
+            op("s", lambda: S.activation(xr[:, 1024 * h:1024 * h + 1024],
+                                         T.xs[:, 0:4096].indirect(T["r16%d" % c][:, 64 * h:64 * h + 64]), AF.Copy),
+               XR + [r("r16")], [r("xr%d" % h)])
+
+        def tail():
+            tt(TI(0), TF(0), P[0][:, 384:512], OP.mult, [r("f0"), r("us")], [r("t0")], [B[0]])
+            ts(TI(1), TI(0), 5, OP.arith_shift_right, [r("t0")], [r("t1")], (), 4095, OP.bitwise_and)
+            tt(TI(2), TI(1), TF(0), OP.add, [r("t1"), r("f0")], [r("t2")])
+            ts(TI(3), TI(2), 4095, OP.bitwise_and, [r("t2")], [r("t3")])
+            tt(T["pk%d" % c][:], TI(3), TF(1), OP.add, [r("t3"), r("f1")], [r("pf")])
+            tt(UF(2), UI(4), T.ite[:, 8 * c:8 * c + 8], OP.add, [r("u4"), "ite"], [r("e")])
+
+        def keys_r():
+            K = P[1][:, 256:384]
+            mm(K, T.ones[0:1, 0:128], T.kt[0:1, :], ["ones", "kt"], B[1], True, False, r("key"))
+            for j in range(16):
+                mm(P[1][:, 256 + j:384:16], xr[:, j:2048:16], T.s16[:], [r("xr0"), r("xr1"), "s16"], B[1], False, False, r("key"))
+
+        def biggest(h):
+            h0, h1 = (0, 2) if h == 9 else (h, h + 1)
+            hs = range(h0, h1)
+            for j in range(16):
+                a = slice(1024 * h0 + j, 1024 * h1, 16)
+                tt(mx[:, a], xr[:, a], P[0][:, 64 * h0:64 * h1], OP.max, [r("xr%d" % h) for h in hs] + [r("x0p")],
+                   [r("mx%d_%d" % (h, j)) for h in hs], [B[0]])
+
+        def keys_m():
+            for j in range(16):
+                mm(P[1][:, 256 + j:384:16], mx[:, j:2048:16], T.s32[:], [r("mx0_%d" % j), r("mx1_%d" % j), "s32"], B[1], False, j == 15, r("key"))
+
+        def least():
+            sc, zs, sb = T["sc%d" % c], T["zs%d" % c], T["sb%d" % c]
+            op("v", lambda: V.tensor_tensor_scan(sc[:], T.rs[:], P[1][:, 256:384], 0.0, OP.max, OP.min), ["rs", r("key")], [r("sc")], [B[1]])
+            cp(UI(5), sc[:, 15:128:16], [r("sc")], [r("u5")])
+            ts(UI(6), UI(5), 15, OP.bitwise_and, [r("u5")], [r("u6")])
+            cp(zs[:, 0:128:16], UI(6), [r("u6")], ["zs%d" % c])
+            op("v", lambda: V.tensor_tensor_scan(sb[:, 0:128], T.keep[:], zs[:], 0.0, OP.mult, OP.add), ["keep", "zs%d" % c], [r("sk")])
+            ts(sb[:, 128:256], sb[:, 0:128], 16.0, OP.is_ge, [r("sk")], [r("sk16")], (), -16.0, OP.mult)
+            L = P[2][:, 0:128]
+            mm(L, T.ones[0:1, 0:128], T.row16[0:1, :], ["ones", "row16"], B[2], True, False, r("l2p"))
+            mm(L, sb[:, 0:128], T.i2[:, 0:128], [r("sk"), "i2"], B[2], False, False, r("l2p"))
+            mm(L, sb[:, 128:256], T.i2[:, 0:128], [r("sk16"), "i2"], B[2], False, True, r("l2p"))
+            tt(sb[:, 256:384], sb[:, 0:128], T.md[:], OP.mult, [r("sk"), "md"], [r("skd")])
+            cp(T["l2%d" % c][:], L, [r("l2p")], [r("l2")], [B[2]])
+
+        def turn_list():
+            sb = T["sb%d" % c]
+            o = P[1][:, 136:144]
+            mm(o, sb[:, 256:384], T.s128[:], [r("skd"), "s128"], B[1], True, False, r("slp"))
+            mm(o, T.i2[:, 0:128], T.it[:], ["i2", "it"], B[1], False, False, r("slp"))
+            mm(o, T.i2[:, 0:128], T.m128[:], ["i2", "m128"], B[1], False, True, r("slp"))
+            cp(LS(1), o, [r("slp")], [r("sl")], [B[1]])
+
+        def gather_q(h):
+            a = slice(1024 * h, 1024 * h + 1024)
+            tt(df[:, a], xr[:].indirect(T["l2%d" % c][:, 64 * h:64 * h + 64]), xw[:, a], OP.subtract,
+               [r("xr0"), r("xr1"), r("l2"), r("xw%d" % h)], [r("df%d" % h)])
+
+        def sizes(h):
+            a = slice(1024 * h, 1024 * h + 1024)
+            op("s", lambda: S.activation(mx[:, a], df[:, a], AF.Abs), [r("df%d" % h)], [r("mx%d_%d" % (h, j)) for j in range(16)])
+            for k in range(16):
+                mm(P[2][:, 128 + 64 * h:192 + 64 * h], T.b0[:, 15 - k:143 - k], mx[:, 1024 * h + k:1024 * h + 1024:16],
+                   ["b0", r("mx%d_%d" % (h, k))], B[2], k == 0, k == 15, r("d2"))
+
+        def halves():
+            for n, (a, rr) in enumerate(((df[:, 15:2048:16], "df"), (xw[:, 15:2048:16], "xw"), (xw[:, 0:2048:16], "xw"))):
+                mm(P[0][:, 128:256], T.hid[:], a, ["hid", r(rr + "0"), r(rr + "1")], B[0], n == 0, n == 2, r("nvp"))
+            ts(T.nvi[:, CW * c:CW * c + CW], P[0][:, 128:256], -0.25, OP.add, [r("nvp")], [r("nv")], [B[0]])
+
+        def unpack():
+            pw, ff = T["pw%d" % c], T["ff%d" % c]
+            ts(T["tl%d" % c][:], pw[:].indirect(LS(1)), 1.0, OP.mult, [r("pw"), r("sl")], [r("tl")], (), 1.0 / 8192 - 2048, OP.add)
+            ts(ff[:, 0:128], T["tl%d" % c][:], 2048.0, OP.add, [r("tl")], [r("tl4")])
+            tt(ff[:, 128:256], pw[:].indirect(LS(1)), ff[:, 0:128], OP.subtract, [r("pw"), r("sl"), r("tl4")], [r("rc")])
+
+        def match():
+            pp = T["pp%d" % c]
+            ts(pp[:, 0:128], P[2][:, 128:256], col(8 if t == 0 else 10), OP.is_le, [r("d2"), "thf" if t == 0 else "thr"], [r("ag")], [B[2]])
+            mm(P[2][:, 256:384], T.tri[:], pp[:, 0:128], ["tri", r("ag")], B[2], True, True, r("pre"))
+            ts(pp[:, 128:256], P[2][:, 256:384], col(4), OP.is_ge, [r("pre"), "k1"], [r("P")], [B[2]])
+            mm(P[1][:, 384:512], T.e8[:], pp[:, 128:256], ["e8", r("P")], B[1], True, True, r("rep"))
+
+        def write_x():
+            src, res = pick(P[1][:, 384:512], [r("rep")], [B[1]], 2, None)
+            tt(UF(3), src, UF(2), OP.mult, [res, r("e")], [r("er")])
+            tt(UF(4), UF(3), T.itf[:, 8 * c:8 * c + 8], OP.add, [r("er"), "itf"], [r("at")])
+            cp(LS(2), UF(4), [r("at")], [r("al")])
+            op("v", lambda: V.tensor_copy(T.xs[:].indirect(LS(2)), T.nvi[:, CW * c:CW * c + CW]), [r("nv"), r("al")], XR)
+
+        def moves():
+            pp = T["pp%d" % c]
+            for m in range(16):
+                mm(P[0][:, 256:264], T.c0[:, 15 - m:143 - m], pp[:, 128 + m:256:16], ["c0", r("P")], B[0], m == 0, False, r("rho"))
+            mm(P[0][:, 256:264], T.i2[:, 0:128], T.it[:], ["i2", "it"], B[0], False, True, r("rho"))
+            Pk = pp[:, 128:256]
+            mm(P[3][:, 0:128], T.m1[:], Pk, ["m1", r("P")], B[3], True, True, r("k1"))
+            mm(P[3][:, 256:384], T.m3[:], Pk, ["m3", r("P")], B[3], True, True, r("k3"))
+            mm(P[3][:, 128:256], T.m2[:], Pk, ["m2", r("P")], B[3], True, False, r("k2"))
+            mm(P[3][:, 128:256], T.ones[0:1, 0:128], T.ones[0:1, 0:128], ["ones"], B[3], False, True, r("k2"))
+
+        def turned():
+            ff = T["ff%d" % c]
+            cp(LS(3), P[0][:, 256:264], [r("rho")], [r("rl")], [B[0]])
+            op("s", lambda: S.activation(ff[:, 256:384], T["ww%d" % c][:].indirect(LS(3)), AF.Copy), [r("ww%d" % n) for n in range(4)] + [r("rl")], [r("wr")])
+
+        def renew():
+            ff, ph = T["ff%d" % c], T["ph%d" % c]
+            tt(ph[:, 128:256], ff[:, 128:256], P[3][:, 0:128], OP.mult, [r("rc"), r("k1")], [r("h1")], [B[3]])
+            tt(ph[:, 256:384], T["tl%d" % c][:], P[3][:, 256:384], OP.mult, [r("tl"), r("k3")], [r("h2")], [B[3]])
+            tt(ph[:, 0:128], ff[:, 256:384], P[3][:, 128:256], OP.mult, [r("wr"), r("k2")], [r("h0")], [B[3]])
+            d = 0 if last else 16 * ((t + 1 + (t + 1) // nrank) - (t + t // nrank))
+            F = P[2][:, 384:512]
+            mm(F, T.an2h[:, 128 - d:256 - d], ph[:, 128:256], ["an2h", r("h1")], B[2], True, False, r("fin"))
+            mm(F, T.i2h[:, 128 - d:256 - d], ph[:, 256:384], ["i2h", r("h2")], B[2], False, False, r("fin"))
+            mm(F, T.i2h[:, 128 - d:256 - d], ph[:, 0:128], ["i2h", r("h0")], B[2], False, True, r("fin"))
+            if last:
+                ts(T.ywf[:, CW * c:CW * c + CW], F, 2048.0, OP.add, [r("fin")], [r("yw")], [B[2]])
+                return
+            wo = T.wo[:, w0:w0 + CW]
+            ts(wo, F, 2048.0, OP.add, [r("fin")], [r("wo%d" % t)], [B[2]])
+            sync_for("gp", [r("wo%d" % t)], [], ())
+            rid, pid, _ = topo.addr(nxt)
+            eng = topo.engines(core, nxt)
+            sem = "ar%d_%d" % (t + 1, c)
+            g.remote_dma(T.wl[:, w0 + 256:w0 + 256 + CW], wo, T.sem[sem], T.sem.sent, pid, rid, topo.mask(core, nxt))
+            total["sent"] = total.get("sent", 0) + len(eng)
+            prev = T.cores[(rank - 1) % nrank]
+            total[sem] = len(topo.engines(prev, core))
+            wrote["wl%d_%d" % (t + 1, c)] = (sem, total[sem], {}, "net")
+
+        def tally():
+            pp = T["pp%d" % c]
+            op("s", lambda: S.activation(pp[:, 256:384], pp[:, 128:256], AF.Copy, accum_out=T.cnt[:, c:c + 1]), [r("P")], [r("cnt"), r("junk")])
+
+        return {"gather_w": gather_w, "wcopy": wcopy, "spin": spin, "pwin": pwin, "weigh": weigh, "relator": relator,
+                "gather_r": gather_r, "tail": tail, "keys_r": keys_r, "biggest": biggest, "keys_m": keys_m, "least": least,
+                "turn_list": turn_list, "gather_q": gather_q, "sizes": sizes, "halves": halves, "unpack": unpack, "match": match,
+                "write_x": write_x, "moves": moves, "turned": turned, "renew": renew, "tally": tally, "spread": spread, "letters": letters}
+
+    def allow():
+        o = T.ps4[:, 264:265]
+        mm(o, T.g8[:], T.cnt[:, 0:1], ["g8", "cnt_0"], "ps4", True, False, "A")
+        mm(o, T.g8[:], T.cnt[:, 1:2], ["g8", "cnt_1"], "ps4", False, True, "A")
+        cp(T.ai[:, 0:1], o, ["A"], ["ai"], ["ps4"])
+        ts(T.aj[:, 0:1], T.ai[:, 0:1], 31, OP.bitwise_and, ["ai"], ["aj"])
+        ts(col(10), T.aj[:, 0:1], 8.0, OP.mult, ["aj", "thf"], ["thr"], (), col(8), OP.add)
+
+    for t in range(VIS):
+        a, b = stages(t, 0), stages(t, 1)
+        once = {"constants_1": constants_1, "constants_2": constants_2, "constants_3": constants_3, "tables": tables, "turns": turns, "rows": rows}
+        for word in (ORDER if t > 0 else FIRST).split():
+            name, _, arg = word.partition(":")
+            if name in once:
+                if t == 0:
+                    once[name]()
+            elif name == "allow":
+                if t > 0:
+                    allow()
+            elif name.endswith(".tally") and t == VIS - 1:
+                pass
+            else:
+                part = (a if name[0] == "a" else b)[name[2:]]
+                if arg == "":
+                    part()
+                elif len(arg) == 1:
+                    part(int(arg))
+                else:
+                    part(int(arg[0]), arg[1])
+
+    dmas("sy", [lambda: SY.dma_start(T.yx[:, 0:2048], T.xs[:, 0:2048]), lambda: SY.dma_start(T.yx[:, 2048:4096], T.xs[:, 2048:4096])],
+         "outx", XR, [])
+    dmas("sy", [lambda: SY.dma_start(T.yw[:], T.ywf[:])], "outw", ["yw_0", "yw_1"], [])
+    for sem, val in total.items():
+        g.wait_ge(T.sem[sem], val)

@@ -3,23 +3,17 @@ from concourse.mybir import dt, AluOpType as OP, AxisListType, ActivationFunctio
 VIS = 6
 NC = 2
 CW = 128
-TURNS = (1, 2, 3, 4, 5, 6, 7, 8, 9, 10, 12, 14, 16)
+CYCLE, FIXED, MM, GATHER, SCATTER = 0.83, 50.0, 0.0, 1.7, 2.0
+OWN, WAKE, LOOK = 120.0, 150.0, 60.0
 
 ORDER = """
-a.wcopy a.gather_w:1v a.gather_w:0s a.weigh a.relator b.gather_w:1s a.spread b.gather_w:0v a.gather_r:0 b.wcopy a.letters a.gather_r:1
-b.weigh a.spin:2 a.tail a.biggest:0 b.spin:0 a.keys_r b.relator a.biggest:1 a.keys_m b.gather_r:0 b.spin:2 b.letters b.gather_r:1
-a.least a.spin:1 a.pwin a.gather_q:1 b.spread a.gather_q:0 allow b.tail b.biggest:9 a.turn_list b.keys_r a.sizes:0 b.keys_m a.sizes:1
-b.least b.spin:3 a.spin:3 a.match a.spin:0 b.gather_q:0 a.moves a.turned b.gather_q:1 a.halves b.pwin a.unpack b.turn_list b.sizes:0
-a.renew b.sizes:1 b.spin:1 b.match b.moves a.write_x a.tally b.unpack b.turned b.renew b.halves b.tally b.write_x
+a.wcopy a.wwin a.gather_w:1v a.gather_w:0s a.weigh a.relator b.gather_w:1s a.spread b.gather_w:0v a.gather_r:0 b.wcopy b.wwin a.letters
+a.gather_r:1 b.weigh a.tail a.pwin a.keys_r b.relator a.biggest:9 a.keys_m b.gather_r:0 b.gather_r:1 b.letters
+a.least a.gather_q:0 b.spread a.gather_q:1 allow b.tail b.pwin a.turn_list b.biggest:9 b.keys_r a.sizes:0 b.keys_m a.sizes:1
+b.least a.halves a.match b.gather_q:0 a.moves a.turned b.gather_q:1 a.unpack b.turn_list b.sizes:0
+a.renew b.sizes:1 b.halves b.match b.moves a.write_x a.tally b.write_x b.unpack b.turned b.renew b.tally
 """
-FIRST = """
-constants_1 constants_3 a.gather_w:0v a.gather_w:1s b.gather_w:1s a.weigh a.relator b.gather_w:0s a.wcopy a.gather_r:0 tables b.weigh
-a.biggest:0 a.gather_r:1 b.relator rows a.biggest:1 a.keys_r a.keys_m a.least b.gather_r:1 turns b.spread b.wcopy a.spread b.gather_r:0
-b.spin:2 constants_2 a.gather_q:0 a.spin:0 a.letters a.tail b.letters b.keys_r a.turn_list b.biggest:9 a.spin:1 a.gather_q:1 b.spin:0
-a.pwin b.keys_m a.spin:2 b.least a.halves a.sizes:1 a.sizes:0 b.spin:3 b.tail a.match a.spin:3 a.moves b.pwin b.gather_q:0 b.turn_list
-b.sizes:0 b.gather_q:1 a.tally a.turned b.halves a.unpack a.renew b.sizes:1 b.match b.spin:1 b.moves a.write_x b.unpack b.turned b.tally
-b.renew b.write_x
-"""
+FIRST = "constants_1 constants_3 tables rows constants_2 " + ORDER.replace(" allow", "")
 
 SCRATCH = {
     "xs": ("sbuf", [128, 4352], "bfloat16"),
@@ -51,15 +45,11 @@ SCRATCH = {
     "g8": ("sbuf", [128, 128], "float32"),
     "b0": ("sbuf", [128, 144], "bfloat16"),
     "c0": ("sbuf", [128, 144], "bfloat16"),
-    "rot": ("sbuf", [128, 1664], "float16"),
-    "mdd": ("sbuf", [128, 160], "bfloat16"),
-    "kt2": ("sbuf", [128, 160], "bfloat16"),
     "m1b": ("sbuf", [128, 128], "bfloat16"),
     "tabr": ("sbuf", [128, 2048], "float32"),
     "tabc": ("sbuf", [128, 2048], "float32"),
     "tabi": ("sbuf", [128, 2048], "int32"),
-    "rota": ("sbuf", [128, 1664], "bfloat16"),
-    "rotb": ("sbuf", [128, 1664], "bfloat16"),
+
     "bm": ("sbuf", [128, 2048], "bfloat16"),
     "bmh": ("sbuf", [128, 2048], "float16"),
     "k2h": ("sbuf", [128, 128], "float16"),
@@ -96,9 +86,10 @@ for _c in range(NC):
         "xr%d" % _c: ("sbuf", [128, 2048], "bfloat16"),
         "mx%d" % _c: ("sbuf", [128, 2048], "bfloat16"),
         "df%d" % _c: ("sbuf", [128, 2048], "bfloat16"),
-        "ww%d" % _c: ("sbuf", [128, 1664], "float32"),
+        "ww%d" % _c: ("sbuf", [128, 2048], "float32"),
         "pw%d" % _c: ("sbuf", [128, 2048], "float32"),
-        "wf%d" % _c: ("sbuf", [128, 128], "float16"),
+        "dw%d" % _c: ("dram", [8, 32, 128], "float32"),
+        "wf%d" % _c: ("sbuf", [128, 128], "float32"),
         "pk%d" % _c: ("sbuf", [128, 128], "float32"),
         "dp%d" % _c: ("dram", [8, 32, 128], "float32"),
         "x0%d" % _c: ("sbuf", [128, 128], "float16"),
@@ -121,7 +112,7 @@ for _b in range(8):
     SCRATCH["ps%d" % _b] = ("psum", [128, 512], "float32")
 
 SEMAPHORES = ["v", "s", "pe", "gp", "sent", "dacc", "ldx", "ldx2", "ldr", "ldw", "ldt", "ldh", "outw", "outx"]
-SEMAPHORES += ["dp%d%d" % (st, c) for st in (1, 2) for c in range(NC)]
+SEMAPHORES += ["d%s%d%d" % (w, st, c) for w in "wp" for st in (1, 2) for c in range(NC)]
 SEMAPHORES += ["ar%d_%d" % (t, c) for t in range(1, VIS) for c in range(NC)]
 
 
@@ -175,33 +166,109 @@ def rank_program(g, core, T, topo):
         for b in banks:
             seen.setdefault(b, {})[q] = tok
 
-    def op(q, call, reads, writes, banks=()):
-        sync_for(q, reads, writes, banks)
-        total[q] = total.get(q, 0) + 1
-        call().then_inc(T.sem[q], 1)
-        note(q, (q, total[q], dict(know[q]), q), reads, writes, banks)
+    nodes = []
 
-    def dmas(q, calls, sem, reads, writes):
-        sync_for(q, reads, writes, ())
-        for call in calls:
-            total[sem] = total.get(sem, 0) + 16
-            call().then_inc(T.sem[sem], 16)
-        note(q, (sem, total[sem], dict(know[q]), "dma"), reads, writes, ())
+    def op(q, call, reads, writes, banks=(), cost=100.0):
+        def emit():
+            sync_for(q, reads, writes, banks)
+            total[q] = total.get(q, 0) + 1
+            call().then_inc(T.sem[q], 1)
+            note(q, (q, total[q], dict(know[q]), q), reads, writes, banks)
+        nodes.append((q, emit, list(reads), list(writes), list(banks), cost, 0.0))
+
+    def dmas(q, calls, sem, reads, writes, extra=2300.0):
+        def emit():
+            sync_for(q, reads, writes, ())
+            for call in calls:
+                total[sem] = total.get(sem, 0) + 16
+                call().then_inc(T.sem[sem], 16)
+            note(q, (sem, total[sem], dict(know[q]), "dma"), reads, writes, ())
+        nodes.append((q, emit, list(reads), list(writes), [], 70.0 * len(calls), extra))
+
+    def span(ap):
+        return ap.shape[1]
+
+    def vcost(n, kind, wide):
+        return {"": FIXED + max(64, n * wide) * CYCLE, "g": FIXED + n * GATHER * CYCLE, "s": FIXED + n * SCATTER * CYCLE}[kind]
 
     def mm(out, lhsT, rhs, reads, bank, start=True, stop=True, tag=None):
-        op("pe", lambda: PE.matmul(out, lhsT, rhs, start, stop), reads, [tag] if tag else [], [bank])
+        op("pe", lambda: PE.matmul(out, lhsT, rhs, start, stop), reads, [tag] if tag else [], [bank], MM + max(64, span(rhs)) * CYCLE * 0.7)
 
-    def tt(out, a, b, o, reads, writes, banks=()):
-        op("v", lambda: V.tensor_tensor(out, a, b, o), reads, writes, banks)
+    def tt(out, a, b, o, reads, writes, banks=(), kind=""):
+        op("v", lambda: V.tensor_tensor(out, a, b, o), reads, writes, banks, vcost(span(out), kind, 1 if banks else 2))
 
-    def ts(out, a, s1, o1, reads, writes, banks=(), s2=None, o2=None):
+    def ts(out, a, s1, o1, reads, writes, banks=(), s2=None, o2=None, kind=""):
+        cost = vcost(span(out), kind, 1)
         if o2 is None:
-            op("v", lambda: V.tensor_scalar(out, a, s1, None, o1), reads, writes, banks)
+            op("v", lambda: V.tensor_scalar(out, a, s1, None, o1), reads, writes, banks, cost)
         else:
-            op("v", lambda: V.tensor_scalar(out, a, s1, s2, o1, o2), reads, writes, banks)
+            op("v", lambda: V.tensor_scalar(out, a, s1, s2, o1, o2), reads, writes, banks, cost)
 
-    def cp(out, a, reads, writes, banks=()):
-        op("v", lambda: V.tensor_copy(out, a), reads, writes, banks)
+    def cp(out, a, reads, writes, banks=(), kind=""):
+        op("v", lambda: V.tensor_copy(out, a), reads, writes, banks, vcost(span(a if kind == "s" else out), kind, 1))
+
+    def act(out, a, f, reads, writes, banks=(), kind="", **more):
+        op("s", lambda: S.activation(out, a, f, **more), reads, writes, banks, vcost(span(out), kind, 1) + 30.0)
+
+    def plan():
+        n = len(nodes)
+        preds = [dict() for _ in range(n)]
+        last, rd, bk = {}, {}, {}
+        for i, (q, _, reads, writes, banks, _, _) in enumerate(nodes):
+            def edge(j, hard):
+                preds[i][j] = preds[i].get(j, False) or hard
+            for x in reads:
+                edge(last[x], True)
+                rd.setdefault(x, []).append(i)
+            for x in writes:
+                if x in last:
+                    edge(last[x], not (q == "pe" and nodes[last[x]][0] == "pe"))
+                for j in rd.get(x, ()):
+                    if j != i:
+                        edge(j, nodes[j][0] != q or q == "sy")
+                last[x], rd[x] = i, []
+            for b in banks:
+                for q2, j in bk.setdefault(b, {}).items():
+                    if j != i and (q2 != q or q == "pe"):
+                        edge(j, q2 != q)
+                bk[b][q] = i
+        succs = [[] for _ in range(n)]
+        left = [len(p) for p in preds]
+        for i, p in enumerate(preds):
+            for j, hard in p.items():
+                succs[j].append((i, hard))
+
+        def lag(j, i, hard):
+            return (nodes[j][6] + (OWN if nodes[j][0] == nodes[i][0] else WAKE)) if hard else 0.0
+        prio = [0.0] * n
+        for i in range(n - 1, -1, -1):
+            prio[i] = nodes[i][5] + max([prio[k] + lag(i, k, hard) for k, hard in succs[i]] + [0.0])
+        ready = {q: [] for q in queue}
+        at = [0.0] * n
+        free = {q: 0.0 for q in queue}
+        for i in range(n):
+            if left[i] == 0:
+                ready[nodes[i][0]].append(i)
+        order = []
+        while len(order) < n:
+            best = None
+            for q, c in ready.items():
+                if c:
+                    t0 = min(max(free[q], at[i]) for i in c)
+                    if best is None or t0 < best[0]:
+                        best = (t0, q)
+            t0, q = best
+            i = max((i for i in ready[q] if max(free[q], at[i]) <= t0 + LOOK), key=lambda z: prio[z] - (max(free[q], at[z]) - t0))
+            ready[q].remove(i)
+            t1 = max(free[q], at[i])
+            free[q] = t1 + nodes[i][5]
+            order.append(i)
+            for k, hard in succs[i]:
+                at[k] = max(at[k], free[q] + lag(i, k, hard) if hard else t1)
+                left[k] -= 1
+                if left[k] == 0:
+                    ready[nodes[k][0]].append(k)
+        return order
 
     dmas("sy", [lambda: SY.dma_start(T.wdi[:], T.wd[:])], "ldw", [], ["wdi"])
     dmas("s", [lambda: S.dma_start(T.xs[:, 0:2048], T.x[:, 0:2048])], "ldx", [], ["x_lo"])
@@ -224,7 +291,7 @@ def rank_program(g, core, T, topo):
     op("v", lambda: V.memset(T.zerf[:], 0.0), [], ["zerf"])
     op("v", lambda: V.memset(T.b0[:], 0.0), [], ["b0"])
     for c in range(NC):
-        op("v", lambda: V.memset(T["zs%d" % c][:], 1.0), [], ["zs%d" % c])
+        op("v", (lambda c: lambda: V.memset(T["zs%d" % c][:], 1.0))(c), [], ["zs%d" % c])
     ts(T.pj[:], T.pi[:], 15, OP.bitwise_and, ["pi"], ["pj"])
     cp(col(0), T.pj[:, 0:1], ["pj"], ["k0"])
     op("gp", lambda: g.iota(T.kt[:], [[0, 8], [1, 16]], 0, 0, allow_small_or_imprecise_dtypes=True), [], ["kt"])
@@ -247,9 +314,6 @@ def rank_program(g, core, T, topo):
         cp(T.tabr[:], T.rts[:], ["rts"], ["tabr"])
         dmas("gp", [lambda: g.dma_start(T.tabc[:], T.tabr[:], accum_op=OP.add)], "dacc", ["tabr", "tabc"], ["tabc"])
 
-    def turns():
-        cp(T.rot[:], T.rotb[:], ["rotb%d" % n for n in range(len(TURNS))], ["rot"])
-
     def rows():
         cp(T.bmh[:], T.bm[:], ["bm%d" % n for n in range(8)], ["bmh"])
 
@@ -270,14 +334,8 @@ def rank_program(g, core, T, topo):
         ts(T.hid[:], T.i2[:, 0:128], 0.5, OP.mult, ["i2"], ["hid"])
 
     def constants_3():
-        op("gp", lambda: g.iota(T.kt2[:], [[0, 10], [1, 16]], 0, 0, allow_small_or_imprecise_dtypes=True), [], ["kt2"])
         for n in range(8):
             sel(T.bm[:, 256 * n:256 * n + 256], T.ones[:], [[-1, 2], [-16, 8], [0, 16]], OP.is_equal, 0.0, -2 * n, 1, ["ones"], ["bm%d" % n])
-        ts(T.mdd[:], T.kt2[:], col(0), OP.is_equal, ["kt2", "k0"], ["mdd"])
-        for n, q in enumerate(TURNS):
-            a = T.rota[:, 128 * n:128 * n + 128]
-            sel(a, T.mdd[:, q:q + 128], [[-16, 8], [0, 16]], OP.is_ge, 0.0, 0, 1, ["mdd"], ["rota%d" % n])
-            sel(T.rotb[:, 128 * n:128 * n + 128], a, [[16, 8], [0, 16]], OP.is_ge, 0.0, 15, -1, ["rota%d" % n], ["rotb%d" % n])
 
     def constants_2():
         cp(col(8), T.thi[:, 0:1], ["thi"], ["thf"])
@@ -288,9 +346,7 @@ def rank_program(g, core, T, topo):
         ts(col(5), col(0), 8.0, OP.is_equal, ["k0"], ["q8"])
         ts(col(6), col(0), 9.0, OP.is_ge, ["k0"], ["q9"], (), 1.0, OP.add)
         ts(col(7), col(5), -8.0, OP.mult, ["q8"], ["q7"])
-        tt(col(11), col(6), col(7), OP.add, ["q9", "q7"], ["qd"])
-        ts(col(12), col(0), 13.0, OP.is_ge, ["k0"], ["q13"])
-        tt(col(9), col(11), col(12), OP.subtract, ["qd", "q13"], ["qc"])
+        tt(col(9), col(6), col(7), OP.add, ["q9", "q7"], ["qc"])
         ts(T.c0[:], T.b0[:], col(9), OP.mult, ["b0", "qc"], ["c0"], (), 128.0, OP.mult)
         ts(T.g8[:], T.ones[:, 0:128], col(5), OP.mult, ["ones", "q8"], ["g8"])
         cp(T.an2h[:], T.an2[:], ["an2"], ["an2h"])
@@ -322,20 +378,13 @@ def rank_program(g, core, T, topo):
             o = xw[:, 1024 * h:1024 * h + 1024]
             i = T.xs[:, 0:4096].indirect(T.wl[:, w0 + 64 * h:w0 + 64 * h + 64])
             if q == "s":
-                op("s", lambda: S.activation(o, i, AF.Copy), XR + [wres], [r("xw%d" % h)])
+                act(o, i, AF.Copy, XR + [wres], [r("xw%d" % h)], kind="g")
             else:
-                op("v", lambda: V.tensor_copy(o, i), XR + [wres], [r("xw%d" % h)])
+                cp(o, i, XR + [wres], [r("xw%d" % h)], kind="g")
 
         def wcopy():
             ts(T["wf%d" % c][:], T.wl[:, w0:w0 + CW], -2048.0, OP.add, [wres], [r("wf")])
 
-        def spin(n):
-            lo, hi = 4 * n, min(4 * n + 4, len(TURNS))
-            for q in range(lo, hi):
-                mm(P[3][:, 128 * (q - lo):128 * (q - lo) + 128], T.rot[:, 128 * q:128 * q + 128], T["wf%d" % c][:],
-                   ["rot", r("wf")], B[3], True, True, r("wsp"))
-            op("s", lambda: S.activation(T["ww%d" % c][:, 128 * lo:128 * hi], P[3][:, 0:128 * (hi - lo)], AF.Copy),
-               [r("wsp")], [r("ww%d" % n)], [B[3]])
 
         def window(kind, src, win, dram, off):
             d, w, s = T[dram], T[win], T[src]
@@ -343,7 +392,10 @@ def rank_program(g, core, T, topo):
             dmas("sy", [lambda: SY.dma_start(d[:, 0:16, :], s[:]), lambda: SY.dma_start(d[:, 16:32, :], s[:])],
                  "d%s1%d" % (kind, c), rs, [r(kind + "d")])
             dmas("sy", [(lambda k: lambda: SY.dma_start(w[k:128:16, :], d[:, k + off:k + off + 16, :]))(k) for k in range(16)],
-                 "d%s2%d" % (kind, c), [r(kind + "d")], [r(kind + "w")])
+                 "d%s2%d" % (kind, c), [r(kind + "d")], [r(kind + "w")], 5000.0)
+
+        def wwin():
+            window("w", "wf%d" % c, "ww%d" % c, "dw%d" % c, 1)
 
         def pwin():
             window("p", "pk%d" % c, "pw%d" % c, "dp%d" % c, 0)
@@ -386,13 +438,12 @@ def rank_program(g, core, T, topo):
                 mm(P[0][:, 384 + m:512:16], T.bmh[:, 128 * m:128 * m + 128], y[:], ["bmh", r("y")], B[0], False, m == 15, r("us"))
 
         def letters():
-            op("s", lambda: S.activation(TF(0), T.tabr[:].indirect(LS(0)), AF.Copy), ["tabr", r("cl")], [r("f0")])
-            op("s", lambda: S.activation(TF(1), T.tabc[:].indirect(LS(0)), AF.Copy, scale=1.0 / 4096), ["tabc", r("cl")], [r("f1")])
+            act(TF(0), T.tabr[:].indirect(LS(0)), AF.Copy, ["tabr", r("cl")], [r("f0")], kind="g")
+            act(TF(1), T.tabc[:].indirect(LS(0)), AF.Copy, ["tabc", r("cl")], [r("f1")], kind="g", scale=1.0 / 4096)
 
         def gather_r(h):
-            op("s", lambda: S.activation(xr[:, 1024 * h:1024 * h + 1024],
-                                         T.xs[:, 0:4096].indirect(T["r16%d" % c][:, 64 * h:64 * h + 64]), AF.Copy),
-               XR + [r("r16")], [r("xr%d" % h)])
+            act(xr[:, 1024 * h:1024 * h + 1024], T.xs[:, 0:4096].indirect(T["r16%d" % c][:, 64 * h:64 * h + 64]), AF.Copy,
+                XR + [r("r16")], [r("xr%d" % h)], kind="g")
 
         def tail():
             tt(TI(0), TF(0), P[0][:, 384:512], OP.mult, [r("f0"), r("us")], [r("t0")], [B[0]])
@@ -446,11 +497,11 @@ def rank_program(g, core, T, topo):
         def gather_q(h):
             a = slice(1024 * h, 1024 * h + 1024)
             tt(df[:, a], xr[:].indirect(T["l2%d" % c][:, 64 * h:64 * h + 64]), xw[:, a], OP.subtract,
-               [r("xr0"), r("xr1"), r("l2"), r("xw%d" % h)], [r("df%d" % h)])
+               [r("xr0"), r("xr1"), r("l2"), r("xw%d" % h)], [r("df%d" % h)], kind="g")
 
         def sizes(h):
             a = slice(1024 * h, 1024 * h + 1024)
-            op("s", lambda: S.activation(mx[:, a], df[:, a], AF.Abs), [r("df%d" % h)], [r("mx%d_%d" % (h, j)) for j in range(16)])
+            act(mx[:, a], df[:, a], AF.Abs, [r("df%d" % h)], [r("mx%d_%d" % (h, j)) for j in range(16)])
             for k in range(16):
                 mm(P[2][:, 128 + 64 * h:192 + 64 * h], T.b0[:, 15 - k:143 - k], mx[:, 1024 * h + k:1024 * h + 1024:16],
                    ["b0", r("mx%d_%d" % (h, k))], B[2], k == 0, k == 15, r("d2"))
@@ -478,7 +529,7 @@ def rank_program(g, core, T, topo):
             tt(UF(3), src, UF(2), OP.mult, [res, r("e")], [r("er")])
             tt(UF(4), UF(3), T.itf[:, 8 * c:8 * c + 8], OP.add, [r("er"), "itf"], [r("at")])
             cp(LS(2), UF(4), [r("at")], [r("al")])
-            op("v", lambda: V.tensor_copy(T.xs[:].indirect(LS(2)), T.nvi[:, CW * c:CW * c + CW]), [r("nv"), r("al")], XR)
+            cp(T.xs[:].indirect(LS(2)), T.nvi[:, CW * c:CW * c + CW], [r("nv"), r("al")], XR, kind="s")
 
         def moves():
             pp = T["pp%d" % c]
@@ -494,7 +545,7 @@ def rank_program(g, core, T, topo):
         def turned():
             ff = T["ff%d" % c]
             cp(LS(3), P[0][:, 256:264], [r("rho")], [r("rl")], [B[0]])
-            op("s", lambda: S.activation(ff[:, 256:384], T["ww%d" % c][:].indirect(LS(3)), AF.Copy), [r("ww%d" % n) for n in range(4)] + [r("rl")], [r("wr")])
+            act(ff[:, 256:384], T["ww%d" % c][:].indirect(LS(3)), AF.Copy, [r("ww"), r("rl")], [r("wr")], kind="g")
 
         def renew():
             ff, ph = T["ff%d" % c], T["ph%d" % c]
@@ -511,21 +562,23 @@ def rank_program(g, core, T, topo):
                 return
             wo = T.wo[:, w0:w0 + CW]
             ts(wo, F, 2048.0, OP.add, [r("fin")], [r("wo%d" % t)], [B[2]])
-            sync_for("gp", [r("wo%d" % t)], [], ())
             rid, pid, _ = topo.addr(nxt)
-            eng = topo.engines(core, nxt)
             sem = "ar%d_%d" % (t + 1, c)
-            g.remote_dma(T.wl[:, w0 + 256:w0 + 256 + CW], wo, T.sem[sem], T.sem.sent, pid, rid, topo.mask(core, nxt))
-            total["sent"] = total.get("sent", 0) + len(eng)
-            prev = T.cores[(rank - 1) % nrank]
-            total[sem] = len(topo.engines(prev, core))
-            wrote["wl%d_%d" % (t + 1, c)] = (sem, total[sem], {}, "net")
+            lands = "wl%d_%d" % (t + 1, c)
+
+            def send():
+                sync_for("gp", [r("wo%d" % t)], [], ())
+                g.remote_dma(T.wl[:, w0 + 256:w0 + 256 + CW], wo, T.sem[sem], T.sem.sent, pid, rid, topo.mask(core, nxt))
+                total["sent"] = total.get("sent", 0) + len(topo.engines(core, nxt))
+                total[sem] = len(topo.engines(T.cores[(rank - 1) % nrank], core))
+                wrote[lands] = (sem, total[sem], {}, "net")
+            nodes.append(("gp", send, [r("wo%d" % t)], [lands], [], 1000.0, 1600.0))
 
         def tally():
             pp = T["pp%d" % c]
             op("s", lambda: S.activation(pp[:, 256:384], pp[:, 128:256], AF.Copy, accum_out=T.cnt[:, c:c + 1]), [r("P")], [r("cnt"), r("junk")])
 
-        return {"gather_w": gather_w, "wcopy": wcopy, "spin": spin, "pwin": pwin, "weigh": weigh, "relator": relator,
+        return {"gather_w": gather_w, "wcopy": wcopy, "wwin": wwin, "pwin": pwin, "weigh": weigh, "relator": relator,
                 "gather_r": gather_r, "tail": tail, "keys_r": keys_r, "biggest": biggest, "keys_m": keys_m, "least": least,
                 "turn_list": turn_list, "gather_q": gather_q, "sizes": sizes, "halves": halves, "unpack": unpack, "match": match,
                 "write_x": write_x, "moves": moves, "turned": turned, "renew": renew, "tally": tally, "spread": spread, "letters": letters}
@@ -540,7 +593,7 @@ def rank_program(g, core, T, topo):
 
     for t in range(VIS):
         a, b = stages(t, 0), stages(t, 1)
-        once = {"constants_1": constants_1, "constants_2": constants_2, "constants_3": constants_3, "tables": tables, "turns": turns, "rows": rows}
+        once = {"constants_1": constants_1, "constants_2": constants_2, "constants_3": constants_3, "tables": tables, "rows": rows}
         for word in (ORDER if t > 0 else FIRST).split():
             name, _, arg = word.partition(":")
             if name in once:
@@ -563,5 +616,7 @@ def rank_program(g, core, T, topo):
     dmas("sy", [lambda: SY.dma_start(T.yx[:, 0:2048], T.xs[:, 0:2048]), lambda: SY.dma_start(T.yx[:, 2048:4096], T.xs[:, 2048:4096])],
          "outx", XR, [])
     dmas("sy", [lambda: SY.dma_start(T.yw[:], T.ywf[:])], "outw", ["yw_0", "yw_1"], [])
+    for i in plan():
+        nodes[i][1]()
     for sem, val in total.items():
         g.wait_ge(T.sem[sem], val)

@@ -3,12 +3,19 @@ from concourse.mybir import dt, AluOpType as OP, AxisListType, ActivationFunctio
 VIS = 6
 NC = 2
 CW = 128
-CYCLE, FIXED, MM, GATHER, SCATTER = 0.83, 50.0, 0.0, 1.7, 2.0
-OWN, WAKE, LOOK = 120.0, 150.0, 60.0
+CYCLE, FIXED, MM, GATHER, SCATTER = 0.83, 20.0, 0.0, 1.7, 3.5
+OWN, WAKE, LOOK = 180.0, 250.0, 60.0
+QV = 1536
+BIAS = {
+    "rows": -8.0, "constants_3": -8.0, "allow": -1.5,
+    "a.wcopy": -1.5, "a.wwin": 0.7, "a.gather_w": -0.7, "a.weigh": -3.0, "a.gather_r": -3.0, "a.letters": 0.7, "a.tail": 0.7, "a.pwin": -1.5,
+    "a.keys_r": 6.0, "a.least": -1.5, "a.turn_list": -3.0, "a.sizes": 0.7, "a.unpack": 3.0, "a.moves": -1.5, "a.tally": -3.0, "a.write_x": 3.0,
+    "b.wcopy": -0.7, "b.gather_w": -6.0, "b.spread": 3.0, "b.gather_r": -0.7, "b.letters": 3.0, "b.pwin": -3.0, "b.turn_list": -6.0,
+    "b.halves": -6.0, "b.unpack": -3.0, "b.turned": 1.5, "b.tally": 3.0, "b.write_x": -3.0}
 
 ORDER = """
 a.wcopy a.wwin a.gather_w:1v a.gather_w:0s a.weigh a.relator b.gather_w:1s a.spread b.gather_w:0v a.gather_r:0 b.wcopy b.wwin a.letters
-a.gather_r:1 b.weigh a.tail a.pwin a.keys_r b.relator a.biggest:9 a.keys_m b.gather_r:0 b.gather_r:1 b.letters
+a.gather_r:1 b.weigh a.tail a.pwin a.keys_r b.relator a.biggest:9 a.keys_m b.gather_r:0 b.gather_r:1v b.letters
 a.least a.gather_q:0 b.spread a.gather_q:1 allow b.tail b.pwin a.turn_list b.biggest:9 b.keys_r a.sizes:0 b.keys_m a.sizes:1
 b.least a.halves a.match b.gather_q:0 a.moves a.turned b.gather_q:1 a.unpack b.turn_list b.sizes:0
 a.renew b.sizes:1 b.halves b.match b.moves a.write_x a.tally b.write_x b.unpack b.turned b.renew b.tally
@@ -34,6 +41,10 @@ SCRATCH = {
     "i2h": ("sbuf", [128, 256], "float16"),
     "an2h": ("sbuf", [128, 256], "float16"),
     "hid": ("sbuf", [128, 128], "bfloat16"),
+    "ni": ("sbuf", [128, 128], "bfloat16"),
+    "wbh": ("sbuf", [128, 128], "bfloat16"),
+    "wbl": ("sbuf", [128, 128], "bfloat16"),
+    "wa": ("sbuf", [128, 2], "int32"),
     "tri": ("sbuf", [128, 128], "bfloat16"),
     "m3": ("sbuf", [128, 128], "bfloat16"),
     "e8": ("sbuf", [128, 128], "bfloat16"),
@@ -167,6 +178,7 @@ def rank_program(g, core, T, topo):
             seen.setdefault(b, {})[q] = tok
 
     nodes = []
+    label, now = [], [""]
 
     def op(q, call, reads, writes, banks=(), cost=100.0):
         def emit():
@@ -243,6 +255,8 @@ def rank_program(g, core, T, topo):
         prio = [0.0] * n
         for i in range(n - 1, -1, -1):
             prio[i] = nodes[i][5] + max([prio[k] + lag(i, k, hard) for k, hard in succs[i]] + [0.0])
+        for i in range(n):
+            prio[i] += 1000.0 * BIAS.get(label[i], 0.0)
         ready = {q: [] for q in queue}
         at = [0.0] * n
         free = {q: 0.0 for q in queue}
@@ -271,17 +285,17 @@ def rank_program(g, core, T, topo):
         return order
 
     dmas("sy", [lambda: SY.dma_start(T.wdi[:], T.wd[:])], "ldw", [], ["wdi"])
-    dmas("s", [lambda: S.dma_start(T.xs[:, 0:2048], T.x[:, 0:2048])], "ldx", [], ["x_lo"])
-    dmas("sy", [lambda: SY.dma_start(T.xs[:, 2048:4096], T.x[:, 2048:4096])], "ldx2", [], ["x_hi"])
+    dmas("s", [lambda: S.dma_start(T.xs[:, 0:2048], T.x[:, 0:2048])], "ldx", [], ["x_lo"], 4000.0)
+    dmas("sy", [lambda: SY.dma_start(T.xs[:, 2048:4096], T.x[:, 2048:4096])], "ldx2", [], ["x_hi"], 4000.0)
     dmas("sy", [lambda: SY.dma_start(T.wti[:, 0:1], T.wt[:])], "ldt", [], ["wti"])
-    dmas("sy", [lambda: SY.dma_start(T.rts[:], T.rt[:])], "ldr", [], ["rts"])
+    dmas("sy", [lambda: SY.dma_start(T.rts[:], T.rt[:])], "ldr", [], ["rts"], 6000.0)
     dmas("sy", [lambda: SY.dma_start(T.thi[:, 0:1], T.th[:])], "ldh", [], ["thi"])
 
     def col(n):
         return T.cols[:, n:n + 1]
 
     def sel(out, in_, pattern, cmp, fill, base, cm, reads, writes):
-        op("gp", lambda: g.affine_select(out, in_, pattern, cmp, fill, base, cm), reads, writes)
+        op("gp", lambda: g.affine_select(out, in_, pattern, cmp, fill, base, cm), reads, writes, (), 170.0 + 2 * span(out) * CYCLE)
 
     op("v", lambda: V.memset(T.ones[:], 1.0), [], ["ones"])
     op("gp", lambda: g.iota(T.pi[:], [[0, 2]], 0, 1), [], ["pi"])
@@ -303,7 +317,11 @@ def rank_program(g, core, T, topo):
     tt(col(3), col(1), col(2), OP.add, ["w1", "w2"], ["w3"])
     ts(T.wt0[:], T.b0[:], col(3), OP.mult, ["b0", "w3"], ["wt0"])
     cp(T.i2h[:], T.i2[:], ["i2"], ["i2h"])
-    ts(T.wb[:], T.blk[:], col(3), OP.mult, ["blk", "w3"], ["wb"])
+    ts(T.wa[:, 0:1], T.wti[:, 0:1], 15, OP.bitwise_and, ["wti"], ["wa"])
+    cp(col(12), T.wa[:, 0:1], ["wa"], ["wlo"])
+    tt(col(11), col(1), col(12), OP.subtract, ["w1", "wlo"], ["whi"])
+    ts(T.wbl[:], T.blk[:], col(12), OP.mult, ["blk", "wlo"], ["wbl"])
+    ts(T.wbh[:], T.blk[:], col(11), OP.mult, ["blk", "whi"], ["wbh"])
     ts(T.md[:], T.kt[:], col(0), OP.is_equal, ["kt", "k0"], ["md"])
     ts(T.k2h[:], T.ones[:, 0:128], 2048.0, OP.mult, ["ones"], ["k2h"])
     cp(T.oneh[:], T.ones[:, 0:128], ["ones"], ["oneh"])
@@ -312,7 +330,7 @@ def rank_program(g, core, T, topo):
         ts(T.tabi[:], T.rts[:], 1, OP.bitwise_and, ["rts"], ["tabi"])
         ts(T.tabc[:], T.tabi[:], -2.0, OP.mult, ["tabi"], ["tabc"], (), -2047.0, OP.add)
         cp(T.tabr[:], T.rts[:], ["rts"], ["tabr"])
-        dmas("gp", [lambda: g.dma_start(T.tabc[:], T.tabr[:], accum_op=OP.add)], "dacc", ["tabr", "tabc"], ["tabc"])
+        dmas("gp", [lambda: g.dma_start(T.tabc[:], T.tabr[:], accum_op=OP.add)], "dacc", ["tabr", "tabc"], ["tabc"], 6000.0)
 
     def rows():
         cp(T.bmh[:], T.bm[:], ["bm%d" % n for n in range(8)], ["bmh"])
@@ -332,6 +350,7 @@ def rank_program(g, core, T, topo):
         ts(T.m128[:], T.ones[:, 0:8], col(0), OP.mult, ["ones", "k0"], ["m128"], (), -128.0, OP.mult)
         ts(T.it[:], T.ihi[:], col(0), OP.add, ["ihi", "k0"], ["it"])
         ts(T.hid[:], T.i2[:, 0:128], 0.5, OP.mult, ["i2"], ["hid"])
+        ts(T.ni[:], T.i2[:, 0:128], -1.0, OP.mult, ["i2"], ["ni"])
 
     def constants_3():
         for n in range(8):
@@ -408,13 +427,15 @@ def rank_program(g, core, T, topo):
 
         def weigh():
             x0 = T["x0%d" % c]
-            cp(x0[:], xw[:, 0:2048:16], [r("xw0"), r("xw1")], [r("x0")])
+            XW = [r("xw0"), r("xw1")]
             if c == 0:
-                mm(P[1][:, 8:136], T.wb[:], x0[:], ["wb", r("x0")], B[1], True, True, r("ub"))
+                mm(P[1][:, 8:136], T.wbh[:], xw[:, 0:2048:16], ["wbh"] + XW, B[1], True, False, r("ub"))
+                mm(P[1][:, 8:136], T.wbl[:], xw[:, 0:2048:16], ["wbl"] + XW, B[1], False, True, r("ub"))
             else:
+                cp(x0[:], xw[:, 0:2048:16], XW, [r("x0")])
                 for m in range(16):
                     mm(P[1][:, 0:8], T.wt0[:, 15 - m:143 - m], x0[:, m:128:16], ["wt0", r("x0")], B[1], m == 0, m == 15, r("uw"))
-            mm(P[0][:, 0:128], T.i2h[:, 0:128], x0[:], ["i2h", r("x0")], B[0], True, True, r("x0p"))
+            mm(P[0][:, 0:128], T.i2[:, 0:128], xw[:, 0:2048:16], ["i2"] + XW, B[0], True, True, r("x0p"))
 
         def relator():
             if c == 0:
@@ -439,11 +460,15 @@ def rank_program(g, core, T, topo):
 
         def letters():
             act(TF(0), T.tabr[:].indirect(LS(0)), AF.Copy, ["tabr", r("cl")], [r("f0")], kind="g")
-            act(TF(1), T.tabc[:].indirect(LS(0)), AF.Copy, ["tabc", r("cl")], [r("f1")], kind="g", scale=1.0 / 4096)
+            act(TF(1), T.tabc[:].indirect(LS(0)), AF.Copy, ["tabc", r("cl")], [r("f1")], kind="g", scale=1.0 / 4096, bias=-2048.0)
 
-        def gather_r(h):
-            act(xr[:, 1024 * h:1024 * h + 1024], T.xs[:, 0:4096].indirect(T["r16%d" % c][:, 64 * h:64 * h + 64]), AF.Copy,
-                XR + [r("r16")], [r("xr%d" % h)], kind="g")
+        def gather_r(h, q="s"):
+            o = xr[:, 1024 * h:1024 * h + 1024]
+            i = T.xs[:, 0:4096].indirect(T["r16%d" % c][:, 64 * h:64 * h + 64])
+            if q == "s":
+                act(o, i, AF.Copy, XR + [r("r16")], [r("xr%d" % h)], kind="g")
+            else:
+                cp(o, i, XR + [r("r16")], [r("xr%d" % h)], kind="g")
 
         def tail():
             tt(TI(0), TF(0), P[0][:, 384:512], OP.mult, [r("f0"), r("us")], [r("t0")], [B[0]])
@@ -465,11 +490,11 @@ def rank_program(g, core, T, topo):
             for j in range(16):
                 a = slice(1024 * h0 + j, 1024 * h1, 16)
                 tt(mx[:, a], xr[:, a], P[0][:, 64 * h0:64 * h1], OP.max, [r("xr%d" % h) for h in hs] + [r("x0p")],
-                   [r("mx%d_%d" % (h, j)) for h in hs], [B[0]])
+                   [r("mx%d_%d" % (h, j)) for h in hs] + [r("mz_%d" % j)] * (h1 - 1), [B[0]])
 
         def keys_m():
             for j in range(16):
-                mm(P[1][:, 256 + j:384:16], mx[:, j:2048:16], T.s32[:], [r("mx0_%d" % j), r("mx1_%d" % j), "s32"], B[1], False, j == 15, r("key"))
+                mm(P[1][:, 256 + j:384:16], mx[:, j:2048:16], T.s32[:], [r("mx0_%d" % j), r("mx1_%d" % j), r("mz_%d" % j), "s32"], B[1], False, j == 15, r("key"))
 
         def least():
             sc, zs, sb = T["sc%d" % c], T["zs%d" % c], T["sb%d" % c]
@@ -495,27 +520,36 @@ def rank_program(g, core, T, topo):
             cp(LS(1), o, [r("slp")], [r("sl")], [B[1]])
 
         def gather_q(h):
-            a = slice(1024 * h, 1024 * h + 1024)
-            tt(df[:, a], xr[:].indirect(T["l2%d" % c][:, 64 * h:64 * h + 64]), xw[:, a], OP.subtract,
+            lo, hi = 1024 * h, (1024, QV)[h]
+            tt(df[:, lo:hi], xr[:].indirect(T["l2%d" % c][:, lo // 16:hi // 16]), xw[:, lo:hi], OP.subtract,
                [r("xr0"), r("xr1"), r("l2"), r("xw%d" % h)], [r("df%d" % h)], kind="g")
+            if h == 1:
+                act(df[:, QV:2048], xr[:].indirect(T["l2%d" % c][:, QV // 16:128]), AF.Copy, [r("xr0"), r("xr1"), r("l2")], [r("df2")], kind="g")
+                o = P[3][:, 0:2048 - QV]
+                mm(o, T.i2[:, 0:128], df[:, QV:2048], ["i2", r("df2")], B[3], True, False, r("dq"))
+                mm(o, T.ni[:], xw[:, QV:2048], ["ni", r("xw1")], B[3], False, True, r("dq"))
+                act(mx[:, QV:2048], o, AF.Abs, [r("dq")], [r("mz_%d" % j) for j in range(16)], [B[3]])
 
         def sizes(h):
-            a = slice(1024 * h, 1024 * h + 1024)
+            a = slice(1024 * h, (1024, QV)[h])
             act(mx[:, a], df[:, a], AF.Abs, [r("df%d" % h)], [r("mx%d_%d" % (h, j)) for j in range(16)])
             for k in range(16):
                 mm(P[2][:, 128 + 64 * h:192 + 64 * h], T.b0[:, 15 - k:143 - k], mx[:, 1024 * h + k:1024 * h + 1024:16],
-                   ["b0", r("mx%d_%d" % (h, k))], B[2], k == 0, k == 15, r("d2"))
+                   ["b0", r("mx%d_%d" % (h, k))] + [r("mz_%d" % k)] * h, B[2], k == 0, k == 15, r("d2"))
 
         def halves():
-            for n, (a, rr) in enumerate(((df[:, 15:2048:16], "df"), (xw[:, 15:2048:16], "xw"), (xw[:, 0:2048:16], "xw"))):
-                mm(P[0][:, 128:256], T.hid[:], a, ["hid", r(rr + "0"), r(rr + "1")], B[0], n == 0, n == 2, r("nvp"))
+            v = 128 + QV // 16
+            XW = [r("xw0"), r("xw1")]
+            mm(P[0][:, 128:256], T.hid[:], xw[:, 0:2048:16], ["hid"] + XW, B[0], True, False, r("nvp"))
+            mm(P[0][:, 128:v], T.hid[:], xw[:, 15:QV:16], ["hid"] + XW, B[0], False, False, r("nvp"))
+            mm(P[0][:, 128:v], T.hid[:], df[:, 15:QV:16], ["hid", r("df0"), r("df1")], B[0], False, False, r("nvp"))
+            mm(P[0][:, v:256], T.hid[:], df[:, QV + 15:2048:16], ["hid", r("df2")], B[0], False, True, r("nvp"))
             ts(T.nvi[:, CW * c:CW * c + CW], P[0][:, 128:256], -0.25, OP.add, [r("nvp")], [r("nv")], [B[0]])
 
         def unpack():
             pw, ff = T["pw%d" % c], T["ff%d" % c]
-            ts(T["tl%d" % c][:], pw[:].indirect(LS(1)), 1.0, OP.mult, [r("pw"), r("sl")], [r("tl")], (), 1.0 / 8192 - 2048, OP.add)
-            ts(ff[:, 0:128], T["tl%d" % c][:], 2048.0, OP.add, [r("tl")], [r("tl4")])
-            tt(ff[:, 128:256], pw[:].indirect(LS(1)), ff[:, 0:128], OP.subtract, [r("pw"), r("sl"), r("tl4")], [r("rc")])
+            ts(T["tl%d" % c][:], pw[:].indirect(LS(1)), 1.0 / 8192, OP.add, [r("pw"), r("sl")], [r("tl")], kind="g")
+            tt(ff[:, 128:256], pw[:].indirect(LS(1)), T["tl%d" % c][:], OP.subtract, [r("pw"), r("sl"), r("tl")], [r("rc")], kind="g")
 
         def match():
             pp = T["pp%d" % c]
@@ -595,6 +629,8 @@ def rank_program(g, core, T, topo):
         a, b = stages(t, 0), stages(t, 1)
         once = {"constants_1": constants_1, "constants_2": constants_2, "constants_3": constants_3, "tables": tables, "rows": rows}
         for word in (ORDER if t > 0 else FIRST).split():
+            label.extend([now[0]] * (len(nodes) - len(label)))
+            now[0] = ("" if t > 0 else "0") + word.partition(":")[0]
             name, _, arg = word.partition(":")
             if name in once:
                 if t == 0:
@@ -616,6 +652,7 @@ def rank_program(g, core, T, topo):
     dmas("sy", [lambda: SY.dma_start(T.yx[:, 0:2048], T.xs[:, 0:2048]), lambda: SY.dma_start(T.yx[:, 2048:4096], T.xs[:, 2048:4096])],
          "outx", XR, [])
     dmas("sy", [lambda: SY.dma_start(T.yw[:], T.ywf[:])], "outw", ["yw_0", "yw_1"], [])
+    label.extend([""] * (len(nodes) - len(label)))
     for i in plan():
         nodes[i][1]()
     for sem, val in total.items():

from concourse.mybir import dt, AluOpType as OP, AxisListType, ActivationFunctionType as AF

VIS = 6
NC = 2
CW = 128
CYCLE, FIXED, MM, GATHER, SCATTER = 0.83, 20.0, 0.0, 1.7, 3.5
OWN, WAKE, LOOK = 180.0, 250.0, 60.0
QV = 1536
BIAS = {
    "rows": -8.0, "constants_3": -8.0, "allow": -1.5,
    "a.wcopy": -1.5, "a.wwin": 0.7, "a.gather_w": -0.7, "a.weigh": -3.0, "a.gather_r": -3.0, "a.letters": 0.7, "a.tail": 0.7, "a.pwin": -1.5,
    "a.keys_r": 6.0, "a.least": -1.5, "a.turn_list": -3.0, "a.sizes": 0.7, "a.unpack": 3.0, "a.moves": -1.5, "a.tally": -3.0, "a.write_x": 3.0,
    "b.wcopy": -0.7, "b.gather_w": -6.0, "b.spread": 3.0, "b.gather_r": -0.7, "b.letters": 3.0, "b.pwin": -3.0, "b.turn_list": -6.0,
    "b.halves": -6.0, "b.unpack": -3.0, "b.turned": 1.5, "b.tally": 3.0, "b.write_x": -3.0}

ORDER = """
a.wcopy a.wwin a.gather_w:1v a.gather_w:0s a.weigh a.relator b.gather_w:1s a.spread b.gather_w:0v a.gather_r:0 b.wcopy b.wwin a.letters
a.gather_r:1 b.weigh a.tail a.pwin a.keys_r b.relator a.biggest:9 a.keys_m b.gather_r:0 b.gather_r:1v b.letters
a.least a.gather_q:0 b.spread a.gather_q:1 allow b.tail b.pwin a.turn_list b.biggest:9 b.keys_r a.sizes:0 b.keys_m a.sizes:1
b.least a.halves a.match b.gather_q:0 a.moves a.turned b.gather_q:1 a.unpack b.turn_list b.sizes:0
a.renew b.sizes:1 b.halves b.match b.moves a.write_x a.tally b.write_x b.unpack b.turned b.renew b.tally
"""
FIRST = "constants_1 constants_3 tables rows constants_2 " + ORDER.replace(" allow", "")

SCRATCH = {
    "xs": ("sbuf", [128, 4352], "bfloat16"),
    "rts": ("sbuf", [128, 2048], "int32"),
    "wdi": ("sbuf", [128, 256], "int32"),
    "wti": ("sbuf", [128, 2], "int32"),
    "thi": ("sbuf", [128, 2], "int32"),
    "wl": ("sbuf", [128, 256 * VIS], "uint16"),
    "wo": ("sbuf", [128, 256 * VIS], "uint16"),
    "ywf": ("sbuf", [128, 256], "float32"),
    "nvi": ("sbuf", [128, 256], "int32"),
    "ones": ("sbuf", [128, 256], "bfloat16"),
    "zerf": ("sbuf", [128, 128], "float32"),
    "blk": ("sbuf", [128, 128], "bfloat16"),
    "blk0": ("sbuf", [128, 128], "bfloat16"),
    "i2": ("sbuf", [128, 256], "bfloat16"),
    "an2": ("sbuf", [128, 256], "bfloat16"),
    "i2h": ("sbuf", [128, 256], "float16"),
    "an2h": ("sbuf", [128, 256], "float16"),
    "hid": ("sbuf", [128, 128], "bfloat16"),
    "ni": ("sbuf", [128, 128], "bfloat16"),
    "wbh": ("sbuf", [128, 128], "bfloat16"),
    "wbl": ("sbuf", [128, 128], "bfloat16"),
    "wa": ("sbuf", [128, 2], "int32"),
    "tri": ("sbuf", [128, 128], "bfloat16"),
    "m3": ("sbuf", [128, 128], "bfloat16"),
    "e8": ("sbuf", [128, 128], "bfloat16"),
    "m1a": ("sbuf", [128, 128], "bfloat16"),
    "m1": ("sbuf", [128, 128], "bfloat16"),
    "m2a": ("sbuf", [128, 128], "bfloat16"),
    "m2b": ("sbuf", [128, 128], "bfloat16"),
    "m2": ("sbuf", [128, 128], "bfloat16"),
    "g8": ("sbuf", [128, 128], "float32"),
    "b0": ("sbuf", [128, 144], "bfloat16"),
    "c0": ("sbuf", [128, 144], "bfloat16"),
    "m1b": ("sbuf", [128, 128], "bfloat16"),
    "tabr": ("sbuf", [128, 2048], "float32"),
    "tabc": ("sbuf", [128, 2048], "float32"),
    "tabi": ("sbuf", [128, 2048], "int32"),

    "bm": ("sbuf", [128, 2048], "bfloat16"),
    "bmh": ("sbuf", [128, 2048], "float16"),
    "k2h": ("sbuf", [128, 128], "float16"),
    "oneh": ("sbuf", [128, 128], "float16"),
    "y0": ("sbuf", [128, 8], "float16"),
    "y1": ("sbuf", [128, 8], "float16"),
    "wt0": ("sbuf", [128, 144], "float16"),
    "wb": ("sbuf", [128, 128], "float16"),
    "s32": ("sbuf", [128, 8], "bfloat16"),
    "s16": ("sbuf", [128, 8], "bfloat16"),
    "s128": ("sbuf", [128, 8], "bfloat16"),
    "kt": ("sbuf", [128, 128], "bfloat16"),
    "row16": ("sbuf", [128, 128], "bfloat16"),
    "md": ("sbuf", [128, 128], "bfloat16"),
    "rs": ("sbuf", [128, 128], "float32"),
    "keep": ("sbuf", [128, 128], "bfloat16"),
    "pi": ("sbuf", [128, 2], "int32"),
    "pj": ("sbuf", [128, 2], "int32"),
    "cols": ("sbuf", [128, 64], "float32"),
    "ihi": ("sbuf", [128, 8], "float32"),
    "it": ("sbuf", [128, 8], "bfloat16"),
    "m128": ("sbuf", [128, 8], "bfloat16"),
    "itg": ("sbuf", [128, 16], "float32"),
    "itf": ("sbuf", [128, 16], "float32"),
    "ite": ("sbuf", [128, 16], "float32"),
    "itd": ("sbuf", [128, 16], "float32"),
    "cnt": ("sbuf", [128, 2], "float32"),
    "ai": ("sbuf", [128, 2], "int32"),
    "aj": ("sbuf", [128, 2], "int32"),
}
for _c in range(NC):
    SCRATCH.update({
        "xw%d" % _c: ("sbuf", [128, 2048], "bfloat16"),
        "xr%d" % _c: ("sbuf", [128, 2048], "bfloat16"),
        "mx%d" % _c: ("sbuf", [128, 2048], "bfloat16"),
        "df%d" % _c: ("sbuf", [128, 2048], "bfloat16"),
        "ww%d" % _c: ("sbuf", [128, 2048], "float32"),
        "pw%d" % _c: ("sbuf", [128, 2048], "float32"),
        "dw%d" % _c: ("dram", [8, 32, 128], "float32"),
        "wf%d" % _c: ("sbuf", [128, 128], "float32"),
        "pk%d" % _c: ("sbuf", [128, 128], "float32"),
        "dp%d" % _c: ("dram", [8, 32, 128], "float32"),
        "x0%d" % _c: ("sbuf", [128, 128], "float16"),
        "ti%d" % _c: ("sbuf", [128, 1024], "int32"),
        "tf%d" % _c: ("sbuf", [128, 512], "float32"),
        "ui%d" % _c: ("sbuf", [128, 64], "int32"),
        "uf%d" % _c: ("sbuf", [128, 64], "float32"),
        "ls%d" % _c: ("sbuf", [128, 64], "uint16"),
        "r16%d" % _c: ("sbuf", [128, 128], "uint16"),
        "l2%d" % _c: ("sbuf", [128, 128], "uint16"),
        "sc%d" % _c: ("sbuf", [128, 128], "float32"),
        "zs%d" % _c: ("sbuf", [128, 128], "bfloat16"),
        "sb%d" % _c: ("sbuf", [128, 384], "bfloat16"),
        "pp%d" % _c: ("sbuf", [128, 384], "bfloat16"),
        "tl%d" % _c: ("sbuf", [128, 128], "int32"),
        "ff%d" % _c: ("sbuf", [128, 384], "float32"),
        "ph%d" % _c: ("sbuf", [128, 384], "float16"),
    })
for _b in range(8):
    SCRATCH["ps%d" % _b] = ("psum", [128, 512], "float32")

SEMAPHORES = ["v", "s", "pe", "gp", "sent", "dacc", "ldx", "ldx2", "ldr", "ldw", "ldt", "ldh", "outw", "outx"]
SEMAPHORES += ["d%s%d%d" % (w, st, c) for w in "wp" for st in (1, 2) for c in range(NC)]
SEMAPHORES += ["ar%d_%d" % (t, c) for t in range(1, VIS) for c in range(NC)]


def rank_program(g, core, T, topo):
    rank = T.rank_of(core)
    if rank is None:
        return
    nrank = len(T.cores)
    nxt = T.cores[(rank + 1) % nrank]
    V, S, PE, SY = g.vector, g.scalar, g.tensor, g.sync
    queue = {"v": V, "s": S, "pe": PE, "gp": g, "sy": SY}
    total = {}
    know = {q: {} for q in queue}
    wrote, seen = {}, {}

    def need(q, tok):
        if tok is None:
            return
        sem, val, clock, _ = tok
        if know[q].get(sem, 0) < val:
            queue[q].wait_ge(T.sem[sem], val)
            for s2, v2 in clock.items():
                if know[q].get(s2, 0) < v2:
                    know[q][s2] = v2
            know[q][sem] = val

    def sync_for(q, reads, writes, banks):
        toks = []
        for r in reads:
            toks.append(wrote[r])
        for w in writes:
            if w in wrote and not (q == "pe" and wrote[w][3] == q):
                toks.append(wrote[w])
            for tok in seen.get(w, {}).values():
                if tok[3] != q or q == "sy":
                    toks.append(tok)
        for b in banks:
            for q2, tok in seen.get(b, {}).items():
                if q2 != q:
                    toks.append(tok)
        toks.sort(key=lambda z: -z[1])
        for tok in toks:
            need(q, tok)

    def note(q, tok, reads, writes, banks):
        for w in writes:
            wrote[w] = tok
            seen[w] = {}
        for r in reads:
            seen.setdefault(r, {})[tok[0]] = tok
        for b in banks:
            seen.setdefault(b, {})[q] = tok

    nodes = []
    label, now = [], [""]

    def op(q, call, reads, writes, banks=(), cost=100.0):
        def emit():
            sync_for(q, reads, writes, banks)
            total[q] = total.get(q, 0) + 1
            call().then_inc(T.sem[q], 1)
            note(q, (q, total[q], dict(know[q]), q), reads, writes, banks)
        nodes.append((q, emit, list(reads), list(writes), list(banks), cost, 0.0))

    def dmas(q, calls, sem, reads, writes, extra=2300.0):
        def emit():
            sync_for(q, reads, writes, ())
            for call in calls:
                total[sem] = total.get(sem, 0) + 16
                call().then_inc(T.sem[sem], 16)
            note(q, (sem, total[sem], dict(know[q]), "dma"), reads, writes, ())
        nodes.append((q, emit, list(reads), list(writes), [], 70.0 * len(calls), extra))

    def span(ap):
        return ap.shape[1]

    def vcost(n, kind, wide):
        return {"": FIXED + max(64, n * wide) * CYCLE, "g": FIXED + n * GATHER * CYCLE, "s": FIXED + n * SCATTER * CYCLE}[kind]

    def mm(out, lhsT, rhs, reads, bank, start=True, stop=True, tag=None):
        op("pe", lambda: PE.matmul(out, lhsT, rhs, start, stop), reads, [tag] if tag else [], [bank], MM + max(64, span(rhs)) * CYCLE * 0.7)

    def tt(out, a, b, o, reads, writes, banks=(), kind=""):
        op("v", lambda: V.tensor_tensor(out, a, b, o), reads, writes, banks, vcost(span(out), kind, 1 if banks else 2))

    def ts(out, a, s1, o1, reads, writes, banks=(), s2=None, o2=None, kind=""):
        cost = vcost(span(out), kind, 1)
        if o2 is None:
            op("v", lambda: V.tensor_scalar(out, a, s1, None, o1), reads, writes, banks, cost)
        else:
            op("v", lambda: V.tensor_scalar(out, a, s1, s2, o1, o2), reads, writes, banks, cost)

    def cp(out, a, reads, writes, banks=(), kind=""):
        op("v", lambda: V.tensor_copy(out, a), reads, writes, banks, vcost(span(a if kind == "s" else out), kind, 1))

    def act(out, a, f, reads, writes, banks=(), kind="", **more):
        op("s", lambda: S.activation(out, a, f, **more), reads, writes, banks, vcost(span(out), kind, 1) + 30.0)

    def plan():
        n = len(nodes)
        preds = [dict() for _ in range(n)]
        last, rd, bk = {}, {}, {}
        for i, (q, _, reads, writes, banks, _, _) in enumerate(nodes):
            def edge(j, hard):
                preds[i][j] = preds[i].get(j, False) or hard
            for x in reads:
                edge(last[x], True)
                rd.setdefault(x, []).append(i)
            for x in writes:
                if x in last:
                    edge(last[x], not (q == "pe" and nodes[last[x]][0] == "pe"))
                for j in rd.get(x, ()):
                    if j != i:
                        edge(j, nodes[j][0] != q or q == "sy")
                last[x], rd[x] = i, []
            for b in banks:
                for q2, j in bk.setdefault(b, {}).items():
                    if j != i and (q2 != q or q == "pe"):
                        edge(j, q2 != q)
                bk[b][q] = i
        succs = [[] for _ in range(n)]
        left = [len(p) for p in preds]
        for i, p in enumerate(preds):
            for j, hard in p.items():
                succs[j].append((i, hard))

        def lag(j, i, hard):
            return (nodes[j][6] + (OWN if nodes[j][0] == nodes[i][0] else WAKE)) if hard else 0.0
        prio = [0.0] * n
        for i in range(n - 1, -1, -1):
            prio[i] = nodes[i][5] + max([prio[k] + lag(i, k, hard) for k, hard in succs[i]] + [0.0])
        for i in range(n):
            prio[i] += 1000.0 * BIAS.get(label[i], 0.0)
        ready = {q: [] for q in queue}
        at = [0.0] * n
        free = {q: 0.0 for q in queue}
        for i in range(n):
            if left[i] == 0:
                ready[nodes[i][0]].append(i)
        order = []
        while len(order) < n:
            best = None
            for q, c in ready.items():
                if c:
                    t0 = min(max(free[q], at[i]) for i in c)
                    if best is None or t0 < best[0]:
                        best = (t0, q)
            t0, q = best
            i = max((i for i in ready[q] if max(free[q], at[i]) <= t0 + LOOK), key=lambda z: prio[z] - (max(free[q], at[z]) - t0))
            ready[q].remove(i)
            t1 = max(free[q], at[i])
            free[q] = t1 + nodes[i][5]
            order.append(i)
            for k, hard in succs[i]:
                at[k] = max(at[k], free[q] + lag(i, k, hard) if hard else t1)
                left[k] -= 1
                if left[k] == 0:
                    ready[nodes[k][0]].append(k)
        return order

    dmas("sy", [lambda: SY.dma_start(T.wdi[:], T.wd[:])], "ldw", [], ["wdi"])
    dmas("s", [lambda: S.dma_start(T.xs[:, 0:2048], T.x[:, 0:2048])], "ldx", [], ["x_lo"], 4000.0)
    dmas("sy", [lambda: SY.dma_start(T.xs[:, 2048:4096], T.x[:, 2048:4096])], "ldx2", [], ["x_hi"], 4000.0)
    dmas("sy", [lambda: SY.dma_start(T.wti[:, 0:1], T.wt[:])], "ldt", [], ["wti"])
    dmas("sy", [lambda: SY.dma_start(T.rts[:], T.rt[:])], "ldr", [], ["rts"], 6000.0)
    dmas("sy", [lambda: SY.dma_start(T.thi[:, 0:1], T.th[:])], "ldh", [], ["thi"])

    def col(n):
        return T.cols[:, n:n + 1]

    def sel(out, in_, pattern, cmp, fill, base, cm, reads, writes):
        op("gp", lambda: g.affine_select(out, in_, pattern, cmp, fill, base, cm), reads, writes, (), 170.0 + 2 * span(out) * CYCLE)

    op("v", lambda: V.memset(T.ones[:], 1.0), [], ["ones"])
    op("gp", lambda: g.iota(T.pi[:], [[0, 2]], 0, 1), [], ["pi"])
    sel(T.blk0[:], T.ones[:, 0:128], [[-16, 8], [0, 16]], OP.is_ge, 0.0, 0, 1, ["ones"], ["blk0"])
    sel(T.blk[:], T.blk0[:], [[16, 8], [0, 16]], OP.is_ge, 0.0, 15, -1, ["blk0"], ["blk"])
    sel(T.i2[:], T.ones[:], [[0, 2], [-1, 128]], OP.is_equal, 0.0, 0, 1, ["ones"], ["i2"])
    op("v", lambda: V.memset(T.zerf[:], 0.0), [], ["zerf"])
    op("v", lambda: V.memset(T.b0[:], 0.0), [], ["b0"])
    for c in range(NC):
        op("v", (lambda c: lambda: V.memset(T["zs%d" % c][:], 1.0))(c), [], ["zs%d" % c])
    ts(T.pj[:], T.pi[:], 15, OP.bitwise_and, ["pi"], ["pj"])
    cp(col(0), T.pj[:, 0:1], ["pj"], ["k0"])
    op("gp", lambda: g.iota(T.kt[:], [[0, 8], [1, 16]], 0, 0, allow_small_or_imprecise_dtypes=True), [], ["kt"])
    sel(T.keep[:], T.ones[:, 0:128], [[0, 8], [1, 16]], OP.not_equal, 0.0, 0, 0, ["ones"], ["keep"])
    cp(T.b0[:, 15:143:16], T.blk[:, 0:128:16], ["blk"], ["b0"])
    cp(T.wl[:, 0:256], T.wdi[:], ["wdi"], ["wl0_0", "wl0_1"])
    cp(col(1), T.wti[:, 0:1], ["wti"], ["w1"])
    ts(col(2), col(1), 2048.0, OP.is_ge, ["w1"], ["w2"], (), -4096.0, OP.mult)
    tt(col(3), col(1), col(2), OP.add, ["w1", "w2"], ["w3"])
    ts(T.wt0[:], T.b0[:], col(3), OP.mult, ["b0", "w3"], ["wt0"])
    cp(T.i2h[:], T.i2[:], ["i2"], ["i2h"])
    ts(T.wa[:, 0:1], T.wti[:, 0:1], 15, OP.bitwise_and, ["wti"], ["wa"])
    cp(col(12), T.wa[:, 0:1], ["wa"], ["wlo"])
    tt(col(11), col(1), col(12), OP.subtract, ["w1", "wlo"], ["whi"])
    ts(T.wbl[:], T.blk[:], col(12), OP.mult, ["blk", "wlo"], ["wbl"])
    ts(T.wbh[:], T.blk[:], col(11), OP.mult, ["blk", "whi"], ["wbh"])
    ts(T.md[:], T.kt[:], col(0), OP.is_equal, ["kt", "k0"], ["md"])
    ts(T.k2h[:], T.ones[:, 0:128], 2048.0, OP.mult, ["ones"], ["k2h"])
    cp(T.oneh[:], T.ones[:, 0:128], ["ones"], ["oneh"])

    def tables():
        ts(T.tabi[:], T.rts[:], 1, OP.bitwise_and, ["rts"], ["tabi"])
        ts(T.tabc[:], T.tabi[:], -2.0, OP.mult, ["tabi"], ["tabc"], (), -2047.0, OP.add)
        cp(T.tabr[:], T.rts[:], ["rts"], ["tabr"])
        dmas("gp", [lambda: g.dma_start(T.tabc[:], T.tabr[:], accum_op=OP.add)], "dacc", ["tabr", "tabc"], ["tabc"], 6000.0)

    def rows():
        cp(T.bmh[:], T.bm[:], ["bm%d" % n for n in range(8)], ["bmh"])

    def constants_1():
        sel(T.rs[:], T.zerf[:], [[0, 8], [1, 16]], OP.not_equal, 524288.0, 0, 0, ["zerf"], ["rs"])
        op("gp", lambda: g.iota(T.row16[:], [[16, 128]], 0, 0, allow_small_or_imprecise_dtypes=True), [], ["row16"])
        op("gp", lambda: g.iota(T.ihi[:], [[16, 8]], 0, 0, allow_small_or_imprecise_dtypes=True), [], ["ihi"])
        op("gp", lambda: g.iota(T.itg[:], [[16, 16]], 0, 0, allow_small_or_imprecise_dtypes=True), [], ["itg"])
        sel(T.tri[:], T.blk[:], [[1, 128]], OP.is_ge, 0.0, 0, -1, ["blk"], ["tri"])
        sel(T.e8[:], T.ones[:, 0:128], [[-16, 8], [0, 16]], OP.is_equal, 0.0, -8, 1, ["ones"], ["e8"])
        sel(T.an2[:], T.ones[:], [[0, 2], [-16, 8], [1, 16]], OP.is_equal, 0.0, -15, 1, ["ones"], ["an2"])
        sel(T.m3[:], T.ones[:, 0:128], [[-16, 8], [1, 8], [0, 2]], OP.is_equal, 0.0, -15, 1, ["ones"], ["m3"])
        ts(T.s32[:], T.blk[:, 0:128:16], 32.0, OP.mult, ["blk"], ["s32"])
        ts(T.s16[:], T.blk[:, 0:128:16], -16.0, OP.mult, ["blk"], ["s16"])
        ts(T.s128[:], T.blk[:, 0:128:16], 128.0, OP.mult, ["blk"], ["s128"])
        ts(T.m128[:], T.ones[:, 0:8], col(0), OP.mult, ["ones", "k0"], ["m128"], (), -128.0, OP.mult)
        ts(T.it[:], T.ihi[:], col(0), OP.add, ["ihi", "k0"], ["it"])
        ts(T.hid[:], T.i2[:, 0:128], 0.5, OP.mult, ["i2"], ["hid"])
        ts(T.ni[:], T.i2[:, 0:128], -1.0, OP.mult, ["i2"], ["ni"])

    def constants_3():
        for n in range(8):
            sel(T.bm[:, 256 * n:256 * n + 256], T.ones[:], [[-1, 2], [-16, 8], [0, 16]], OP.is_equal, 0.0, -2 * n, 1, ["ones"], ["bm%d" % n])

    def constants_2():
        cp(col(8), T.thi[:, 0:1], ["thi"], ["thf"])
        ts(col(4), col(0), 1.0, OP.add, ["k0"], ["k1"])
        ts(T.itf[:], T.itg[:], col(0), OP.add, ["itg", "k0"], ["itf"], (), 4096.0, OP.add)
        ts(T.itd[:], T.itg[:], col(0), OP.add, ["itg", "k0"], ["itd"], (), 15.0, OP.mult)
        ts(T.ite[:], T.itd[:], -4096.0, OP.add, ["itd"], ["ite"])
        ts(col(5), col(0), 8.0, OP.is_equal, ["k0"], ["q8"])
        ts(col(6), col(0), 9.0, OP.is_ge, ["k0"], ["q9"], (), 1.0, OP.add)
        ts(col(7), col(5), -8.0, OP.mult, ["q8"], ["q7"])
        tt(col(9), col(6), col(7), OP.add, ["q9", "q7"], ["qc"])
        ts(T.c0[:], T.b0[:], col(9), OP.mult, ["b0", "qc"], ["c0"], (), 128.0, OP.mult)
        ts(T.g8[:], T.ones[:, 0:128], col(5), OP.mult, ["ones", "q8"], ["g8"])
        cp(T.an2h[:], T.an2[:], ["an2"], ["an2h"])
        tt(T.m1a[:], T.e8[:], T.i2[:, 0:128], OP.subtract, ["e8", "i2"], ["m1a"])
        tt(T.m2a[:], T.an2[:, 0:128], T.e8[:], OP.subtract, ["an2", "e8"], ["m2a"])
        sel(T.m1b[:], T.m1a[:], [[0, 8], [1, 16]], OP.is_ge, 0.0, -8, 0, ["m1a"], ["m1b"])
        ts(T.m1[:], T.m1b[:], 4096.0, OP.mult, ["m1b"], ["m1"])
        sel(T.m2b[:], T.m2a[:], [[0, 8], [-1, 16]], OP.is_ge, 0.0, 7, 0, ["m2a"], ["m2b"])
        tt(T.m2[:], T.m2b[:], T.m3[:], OP.subtract, ["m2b", "m3"], ["m2"])

    XR = ["x_lo", "x_hi"]

    def stages(t, c):
        B = ["ps%d" % (4 * c + b) for b in range(4)]
        P = [T[b] for b in B]
        r = lambda name: "%s_%d" % (name, c)
        xw, xr, mx, df = T["xw%d" % c], T["xr%d" % c], T["mx%d" % c], T["df%d" % c]
        ti, tf, ui, uf, ls = T["ti%d" % c], T["tf%d" % c], T["ui%d" % c], T["uf%d" % c], T["ls%d" % c]
        w0 = 256 * t + CW * c
        wres = "wl%d_%d" % (t, c)
        TI = lambda n: ti[:, 128 * n:128 * n + 128]
        TF = lambda n: tf[:, 128 * n:128 * n + 128]
        UI = lambda n: ui[:, 8 * n:8 * n + 8]
        UF = lambda n: uf[:, 8 * n:8 * n + 8]
        LS = lambda n: ls[:, 8 * n:8 * n + 8]
        last = t == VIS - 1

        def gather_w(h, q):
            o = xw[:, 1024 * h:1024 * h + 1024]
            i = T.xs[:, 0:4096].indirect(T.wl[:, w0 + 64 * h:w0 + 64 * h + 64])
            if q == "s":
                act(o, i, AF.Copy, XR + [wres], [r("xw%d" % h)], kind="g")
            else:
                cp(o, i, XR + [wres], [r("xw%d" % h)], kind="g")

        def wcopy():
            ts(T["wf%d" % c][:], T.wl[:, w0:w0 + CW], -2048.0, OP.add, [wres], [r("wf")])


        def window(kind, src, win, dram, off):
            d, w, s = T[dram], T[win], T[src]
            rs = [r(kind + "f")]
            dmas("sy", [lambda: SY.dma_start(d[:, 0:16, :], s[:]), lambda: SY.dma_start(d[:, 16:32, :], s[:])],
                 "d%s1%d" % (kind, c), rs, [r(kind + "d")])
            dmas("sy", [(lambda k: lambda: SY.dma_start(w[k:128:16, :], d[:, k + off:k + off + 16, :]))(k) for k in range(16)],
                 "d%s2%d" % (kind, c), [r(kind + "d")], [r(kind + "w")], 5000.0)

        def wwin():
            window("w", "wf%d" % c, "ww%d" % c, "dw%d" % c, 1)

        def pwin():
            window("p", "pk%d" % c, "pw%d" % c, "dp%d" % c, 0)

        def pick(src, srcs, banks, tmp, out):
            a, b2 = TF(tmp), TF(tmp + 1)
            tt(a, src, T.md[:], OP.mult, srcs + ["md"], [r("f%d" % tmp)], banks)
            op("v", lambda: V.tensor_tensor_scan(b2, T.keep[:], a, 0.0, OP.mult, OP.add), ["keep", r("f%d" % tmp)], [r("f%d" % (tmp + 1))])
            return tf[:, 128 * tmp + 143:128 * tmp + 256:16], r("f%d" % (tmp + 1))

        def weigh():
            x0 = T["x0%d" % c]
            XW = [r("xw0"), r("xw1")]
            if c == 0:
                mm(P[1][:, 8:136], T.wbh[:], xw[:, 0:2048:16], ["wbh"] + XW, B[1], True, False, r("ub"))
                mm(P[1][:, 8:136], T.wbl[:], xw[:, 0:2048:16], ["wbl"] + XW, B[1], False, True, r("ub"))
            else:
                cp(x0[:], xw[:, 0:2048:16], XW, [r("x0")])
                for m in range(16):
                    mm(P[1][:, 0:8], T.wt0[:, 15 - m:143 - m], x0[:, m:128:16], ["wt0", r("x0")], B[1], m == 0, m == 15, r("uw"))
            mm(P[0][:, 0:128], T.i2[:, 0:128], xw[:, 0:2048:16], ["i2"] + XW, B[0], True, True, r("x0p"))

        def relator():
            if c == 0:
                src, res = pick(P[1][:, 8:136], [r("ub")], [B[1]], 0, None)
                cp(UI(0), src, [res], [r("u0")])
            else:
                cp(UI(0), P[1][:, 0:8], [r("uw")], [r("u0")], [B[1]])
            ts(UI(1), UI(0), 4095, OP.bitwise_and, [r("u0")], [r("u1")])
            ts(T["y%d" % c][:], UI(1), -2048.0, OP.add, [r("u1")], [r("y")])
            ts(UF(1), UI(1), 3232.0, OP.add, [r("u1")], [r("uz")])
            tt(UI(2), T["y%d" % c][:], UF(1), OP.mult, [r("y"), r("uz")], [r("u2")])
            ts(UI(3), UI(2), 5, OP.arith_shift_right, [r("u2")], [r("u3")], (), 2047, OP.bitwise_and)
            cp(LS(0), UI(3), [r("u3")], [r("cl")])
            cp(T["r16%d" % c][:], T.rts[:].indirect(LS(0)), ["rts", r("cl")], [r("r16")])
            ts(UI(4), UI(1), 15, OP.bitwise_and, [r("u1")], [r("u4")])

        def spread():
            y = T["y%d" % c]
            mm(P[0][:, 384:512], T.k2h[0:1, :], T.oneh[0:1, :], ["k2h", "oneh"], B[0], True, False, r("us"))
            for m in range(16):
                mm(P[0][:, 384 + m:512:16], T.bmh[:, 128 * m:128 * m + 128], y[:], ["bmh", r("y")], B[0], False, m == 15, r("us"))

        def letters():
            act(TF(0), T.tabr[:].indirect(LS(0)), AF.Copy, ["tabr", r("cl")], [r("f0")], kind="g")
            act(TF(1), T.tabc[:].indirect(LS(0)), AF.Copy, ["tabc", r("cl")], [r("f1")], kind="g", scale=1.0 / 4096, bias=-2048.0)

        def gather_r(h, q="s"):
            o = xr[:, 1024 * h:1024 * h + 1024]
            i = T.xs[:, 0:4096].indirect(T["r16%d" % c][:, 64 * h:64 * h + 64])
            if q == "s":
                act(o, i, AF.Copy, XR + [r("r16")], [r("xr%d" % h)], kind="g")
            else:
                cp(o, i, XR + [r("r16")], [r("xr%d" % h)], kind="g")

        def tail():
            tt(TI(0), TF(0), P[0][:, 384:512], OP.mult, [r("f0"), r("us")], [r("t0")], [B[0]])
            ts(TI(1), TI(0), 5, OP.arith_shift_right, [r("t0")], [r("t1")], (), 4095, OP.bitwise_and)
            tt(TI(2), TI(1), TF(0), OP.add, [r("t1"), r("f0")], [r("t2")])
            ts(TI(3), TI(2), 4095, OP.bitwise_and, [r("t2")], [r("t3")])
            tt(T["pk%d" % c][:], TI(3), TF(1), OP.add, [r("t3"), r("f1")], [r("pf")])
            tt(UF(2), UI(4), T.ite[:, 8 * c:8 * c + 8], OP.add, [r("u4"), "ite"], [r("e")])

        def keys_r():
            K = P[1][:, 256:384]
            mm(K, T.ones[0:1, 0:128], T.kt[0:1, :], ["ones", "kt"], B[1], True, False, r("key"))
            for j in range(16):
                mm(P[1][:, 256 + j:384:16], xr[:, j:2048:16], T.s16[:], [r("xr0"), r("xr1"), "s16"], B[1], False, False, r("key"))

        def biggest(h):
            h0, h1 = (0, 2) if h == 9 else (h, h + 1)
            hs = range(h0, h1)
            for j in range(16):
                a = slice(1024 * h0 + j, 1024 * h1, 16)
                tt(mx[:, a], xr[:, a], P[0][:, 64 * h0:64 * h1], OP.max, [r("xr%d" % h) for h in hs] + [r("x0p")],
                   [r("mx%d_%d" % (h, j)) for h in hs] + [r("mz_%d" % j)] * (h1 - 1), [B[0]])

        def keys_m():
            for j in range(16):
                mm(P[1][:, 256 + j:384:16], mx[:, j:2048:16], T.s32[:], [r("mx0_%d" % j), r("mx1_%d" % j), r("mz_%d" % j), "s32"], B[1], False, j == 15, r("key"))

        def least():
            sc, zs, sb = T["sc%d" % c], T["zs%d" % c], T["sb%d" % c]
            op("v", lambda: V.tensor_tensor_scan(sc[:], T.rs[:], P[1][:, 256:384], 0.0, OP.max, OP.min), ["rs", r("key")], [r("sc")], [B[1]])
            cp(UI(5), sc[:, 15:128:16], [r("sc")], [r("u5")])
            ts(UI(6), UI(5), 15, OP.bitwise_and, [r("u5")], [r("u6")])
            cp(zs[:, 0:128:16], UI(6), [r("u6")], ["zs%d" % c])
            op("v", lambda: V.tensor_tensor_scan(sb[:, 0:128], T.keep[:], zs[:], 0.0, OP.mult, OP.add), ["keep", "zs%d" % c], [r("sk")])
            ts(sb[:, 128:256], sb[:, 0:128], 16.0, OP.is_ge, [r("sk")], [r("sk16")], (), -16.0, OP.mult)
            L = P[2][:, 0:128]
            mm(L, T.ones[0:1, 0:128], T.row16[0:1, :], ["ones", "row16"], B[2], True, False, r("l2p"))
            mm(L, sb[:, 0:128], T.i2[:, 0:128], [r("sk"), "i2"], B[2], False, False, r("l2p"))
            mm(L, sb[:, 128:256], T.i2[:, 0:128], [r("sk16"), "i2"], B[2], False, True, r("l2p"))
            tt(sb[:, 256:384], sb[:, 0:128], T.md[:], OP.mult, [r("sk"), "md"], [r("skd")])
            cp(T["l2%d" % c][:], L, [r("l2p")], [r("l2")], [B[2]])

        def turn_list():
            sb = T["sb%d" % c]
            o = P[1][:, 136:144]
            mm(o, sb[:, 256:384], T.s128[:], [r("skd"), "s128"], B[1], True, False, r("slp"))
            mm(o, T.i2[:, 0:128], T.it[:], ["i2", "it"], B[1], False, False, r("slp"))
            mm(o, T.i2[:, 0:128], T.m128[:], ["i2", "m128"], B[1], False, True, r("slp"))
            cp(LS(1), o, [r("slp")], [r("sl")], [B[1]])

        def gather_q(h):
            lo, hi = 1024 * h, (1024, QV)[h]
            tt(df[:, lo:hi], xr[:].indirect(T["l2%d" % c][:, lo // 16:hi // 16]), xw[:, lo:hi], OP.subtract,
               [r("xr0"), r("xr1"), r("l2"), r("xw%d" % h)], [r("df%d" % h)], kind="g")
            if h == 1:
                act(df[:, QV:2048], xr[:].indirect(T["l2%d" % c][:, QV // 16:128]), AF.Copy, [r("xr0"), r("xr1"), r("l2")], [r("df2")], kind="g")
                o = P[3][:, 0:2048 - QV]
                mm(o, T.i2[:, 0:128], df[:, QV:2048], ["i2", r("df2")], B[3], True, False, r("dq"))
                mm(o, T.ni[:], xw[:, QV:2048], ["ni", r("xw1")], B[3], False, True, r("dq"))
                act(mx[:, QV:2048], o, AF.Abs, [r("dq")], [r("mz_%d" % j) for j in range(16)], [B[3]])

        def sizes(h):
            a = slice(1024 * h, (1024, QV)[h])
            act(mx[:, a], df[:, a], AF.Abs, [r("df%d" % h)], [r("mx%d_%d" % (h, j)) for j in range(16)])
            for k in range(16):
                mm(P[2][:, 128 + 64 * h:192 + 64 * h], T.b0[:, 15 - k:143 - k], mx[:, 1024 * h + k:1024 * h + 1024:16],
                   ["b0", r("mx%d_%d" % (h, k))] + [r("mz_%d" % k)] * h, B[2], k == 0, k == 15, r("d2"))

        def halves():
            v = 128 + QV // 16
            XW = [r("xw0"), r("xw1")]
            mm(P[0][:, 128:256], T.hid[:], xw[:, 0:2048:16], ["hid"] + XW, B[0], True, False, r("nvp"))
            mm(P[0][:, 128:v], T.hid[:], xw[:, 15:QV:16], ["hid"] + XW, B[0], False, False, r("nvp"))
            mm(P[0][:, 128:v], T.hid[:], df[:, 15:QV:16], ["hid", r("df0"), r("df1")], B[0], False, False, r("nvp"))
            mm(P[0][:, v:256], T.hid[:], df[:, QV + 15:2048:16], ["hid", r("df2")], B[0], False, True, r("nvp"))
            ts(T.nvi[:, CW * c:CW * c + CW], P[0][:, 128:256], -0.25, OP.add, [r("nvp")], [r("nv")], [B[0]])

        def unpack():
            pw, ff = T["pw%d" % c], T["ff%d" % c]
            ts(T["tl%d" % c][:], pw[:].indirect(LS(1)), 1.0 / 8192, OP.add, [r("pw"), r("sl")], [r("tl")], kind="g")
            tt(ff[:, 128:256], pw[:].indirect(LS(1)), T["tl%d" % c][:], OP.subtract, [r("pw"), r("sl"), r("tl")], [r("rc")], kind="g")

        def match():
            pp = T["pp%d" % c]
            ts(pp[:, 0:128], P[2][:, 128:256], col(8 if t == 0 else 10), OP.is_le, [r("d2"), "thf" if t == 0 else "thr"], [r("ag")], [B[2]])
            mm(P[2][:, 256:384], T.tri[:], pp[:, 0:128], ["tri", r("ag")], B[2], True, True, r("pre"))
            ts(pp[:, 128:256], P[2][:, 256:384], col(4), OP.is_ge, [r("pre"), "k1"], [r("P")], [B[2]])
            mm(P[1][:, 384:512], T.e8[:], pp[:, 128:256], ["e8", r("P")], B[1], True, True, r("rep"))

        def write_x():
            src, res = pick(P[1][:, 384:512], [r("rep")], [B[1]], 2, None)
            tt(UF(3), src, UF(2), OP.mult, [res, r("e")], [r("er")])
            tt(UF(4), UF(3), T.itf[:, 8 * c:8 * c + 8], OP.add, [r("er"), "itf"], [r("at")])
            cp(LS(2), UF(4), [r("at")], [r("al")])
            cp(T.xs[:].indirect(LS(2)), T.nvi[:, CW * c:CW * c + CW], [r("nv"), r("al")], XR, kind="s")

        def moves():
            pp = T["pp%d" % c]
            for m in range(16):
                mm(P[0][:, 256:264], T.c0[:, 15 - m:143 - m], pp[:, 128 + m:256:16], ["c0", r("P")], B[0], m == 0, False, r("rho"))
            mm(P[0][:, 256:264], T.i2[:, 0:128], T.it[:], ["i2", "it"], B[0], False, True, r("rho"))
            Pk = pp[:, 128:256]
            mm(P[3][:, 0:128], T.m1[:], Pk, ["m1", r("P")], B[3], True, True, r("k1"))
            mm(P[3][:, 256:384], T.m3[:], Pk, ["m3", r("P")], B[3], True, True, r("k3"))
            mm(P[3][:, 128:256], T.m2[:], Pk, ["m2", r("P")], B[3], True, False, r("k2"))
            mm(P[3][:, 128:256], T.ones[0:1, 0:128], T.ones[0:1, 0:128], ["ones"], B[3], False, True, r("k2"))

        def turned():
            ff = T["ff%d" % c]
            cp(LS(3), P[0][:, 256:264], [r("rho")], [r("rl")], [B[0]])
            act(ff[:, 256:384], T["ww%d" % c][:].indirect(LS(3)), AF.Copy, [r("ww"), r("rl")], [r("wr")], kind="g")

        def renew():
            ff, ph = T["ff%d" % c], T["ph%d" % c]
            tt(ph[:, 128:256], ff[:, 128:256], P[3][:, 0:128], OP.mult, [r("rc"), r("k1")], [r("h1")], [B[3]])
            tt(ph[:, 256:384], T["tl%d" % c][:], P[3][:, 256:384], OP.mult, [r("tl"), r("k3")], [r("h2")], [B[3]])
            tt(ph[:, 0:128], ff[:, 256:384], P[3][:, 128:256], OP.mult, [r("wr"), r("k2")], [r("h0")], [B[3]])
            d = 0 if last else 16 * ((t + 1 + (t + 1) // nrank) - (t + t // nrank))
            F = P[2][:, 384:512]
            mm(F, T.an2h[:, 128 - d:256 - d], ph[:, 128:256], ["an2h", r("h1")], B[2], True, False, r("fin"))
            mm(F, T.i2h[:, 128 - d:256 - d], ph[:, 256:384], ["i2h", r("h2")], B[2], False, False, r("fin"))
            mm(F, T.i2h[:, 128 - d:256 - d], ph[:, 0:128], ["i2h", r("h0")], B[2], False, True, r("fin"))
            if last:
                ts(T.ywf[:, CW * c:CW * c + CW], F, 2048.0, OP.add, [r("fin")], [r("yw")], [B[2]])
                return
            wo = T.wo[:, w0:w0 + CW]
            ts(wo, F, 2048.0, OP.add, [r("fin")], [r("wo%d" % t)], [B[2]])
            rid, pid, _ = topo.addr(nxt)
            sem = "ar%d_%d" % (t + 1, c)
            lands = "wl%d_%d" % (t + 1, c)

            def send():
                sync_for("gp", [r("wo%d" % t)], [], ())
                g.remote_dma(T.wl[:, w0 + 256:w0 + 256 + CW], wo, T.sem[sem], T.sem.sent, pid, rid, topo.mask(core, nxt))
                total["sent"] = total.get("sent", 0) + len(topo.engines(core, nxt))
                total[sem] = len(topo.engines(T.cores[(rank - 1) % nrank], core))
                wrote[lands] = (sem, total[sem], {}, "net")
            nodes.append(("gp", send, [r("wo%d" % t)], [lands], [], 1000.0, 1600.0))

        def tally():
            pp = T["pp%d" % c]
            op("s", lambda: S.activation(pp[:, 256:384], pp[:, 128:256], AF.Copy, accum_out=T.cnt[:, c:c + 1]), [r("P")], [r("cnt"), r("junk")])

        return {"gather_w": gather_w, "wcopy": wcopy, "wwin": wwin, "pwin": pwin, "weigh": weigh, "relator": relator,
                "gather_r": gather_r, "tail": tail, "keys_r": keys_r, "biggest": biggest, "keys_m": keys_m, "least": least,
                "turn_list": turn_list, "gather_q": gather_q, "sizes": sizes, "halves": halves, "unpack": unpack, "match": match,
                "write_x": write_x, "moves": moves, "turned": turned, "renew": renew, "tally": tally, "spread": spread, "letters": letters}

    def allow():
        o = T.ps4[:, 264:265]
        mm(o, T.g8[:], T.cnt[:, 0:1], ["g8", "cnt_0"], "ps4", True, False, "A")
        mm(o, T.g8[:], T.cnt[:, 1:2], ["g8", "cnt_1"], "ps4", False, True, "A")
        cp(T.ai[:, 0:1], o, ["A"], ["ai"], ["ps4"])
        ts(T.aj[:, 0:1], T.ai[:, 0:1], 31, OP.bitwise_and, ["ai"], ["aj"])
        ts(col(10), T.aj[:, 0:1], 8.0, OP.mult, ["aj", "thf"], ["thr"], (), col(8), OP.add)

    for t in range(VIS):
        a, b = stages(t, 0), stages(t, 1)
        once = {"constants_1": constants_1, "constants_2": constants_2, "constants_3": constants_3, "tables": tables, "rows": rows}
        for word in (ORDER if t > 0 else FIRST).split():
            label.extend([now[0]] * (len(nodes) - len(label)))
            now[0] = ("" if t > 0 else "0") + word.partition(":")[0]
            name, _, arg = word.partition(":")
            if name in once:
                if t == 0:
                    once[name]()
            elif name == "allow":
                if t > 0:
                    allow()
            elif name.endswith(".tally") and t == VIS - 1:
                pass
            else:
                part = (a if name[0] == "a" else b)[name[2:]]
                if arg == "":
                    part()
                elif len(arg) == 1:
                    part(int(arg))
                else:
                    part(int(arg[0]), arg[1])

    dmas("sy", [lambda: SY.dma_start(T.yx[:, 0:2048], T.xs[:, 0:2048]), lambda: SY.dma_start(T.yx[:, 2048:4096], T.xs[:, 2048:4096])],
         "outx", XR, [])
    dmas("sy", [lambda: SY.dma_start(T.yw[:], T.ywf[:])], "outw", ["yw_0", "yw_1"], [])
    label.extend([""] * (len(nodes) - len(label)))
    for i in plan():
        nodes[i][1]()
    for sem, val in total.items():
        g.wait_ge(T.sem[sem], val)
